import numpy as np, ml_dtypes
CORES = [25,29,65,69,153,157,193,197]
N = 8
import mx_ref
BF = ml_dtypes.bfloat16
def entries(a):
    return np.ascontiguousarray(a.T).reshape(-1)
def table(e):
    return np.ascontiguousarray(np.reshape(e, (-1, 16)).T).astype(np.int32)
def pick(q, e):
    c = np.concatenate([q[0].reshape(128, -1, 4), np.zeros((128, 1, 4), np.uint8)], axis=1); s = np.concatenate([q[1], np.ones((16, 1), np.uint8)], axis=1)
    return (np.ascontiguousarray(c[:, e].reshape(128, -1)), np.ascontiguousarray(s[:, e]))
def join(*qs):
    return (np.concatenate([q[0] for q in qs], axis=1), np.concatenate([q[1] for q in qs], axis=1))
def put(q, e, v):
    c, s = q[0].reshape(128, -1, 4).copy(), q[1].copy(); c[:, e] = v[0].reshape(128, -1, 4); s[:, e] = v[1]
    return (c.reshape(128, -1), s)
def pk(c, s):
    return (np.ascontiguousarray(c), mx_ref.live(s))
def emit(q):
    return q[0], q[1]
def decode(q):
    o = []
    for b in range(4):
        e = np.zeros((128, 128, 4), np.float32); e[np.arange(128), np.arange(128), b] = 1
        o.append(mx_ref.matmul(mx_ref.quantize(e.reshape(128, 512).astype(BF)), q))
    return np.stack(o, axis=2).reshape(128, -1)
def cut(t, i, w=512):
    return t[:, w * i:w * i + w]
def f(rng, *shape):
    return mx_ref.flush((rng.standard_normal(shape, dtype=np.float32) * np.exp2(rng.integers(-2, 3, shape[:-1] + (1,)))).astype(BF))
def wide(rng, *shape, cols=0):
    v = rng.standard_normal(shape, dtype=np.float32) * np.exp2(rng.integers(-12, 13, shape)).astype(np.float32)
    if cols: v *= np.repeat(np.exp2(rng.integers(-cols, cols + 1, shape[:-2] + (1, shape[-1] // 4))) * (rng.random(shape[:-2] + (1, shape[-1] // 4)) > 0.0625), 4, axis=-1).astype(np.float32)
    return mx_ref.flush(v.astype(BF))
V, E, PAIR, CAP, R, O = 32, 128, 16, 8, 3, 2
def lift(v):
    v = np.array(v, np.float32)
    v[np.abs(v) < np.float32(2.0 ** -12)] = 0
    return v.astype(BF)
def lay(back):
    return np.stack([table(back[E * r:E * r + E]) for r in range(N)])
def links(rng):
    back = np.zeros(N * E, int)
    part = [rng.permutation(E).reshape(N, PAIR) + E * r for r in range(N)]
    for r in range(N):
        for h in range(r, N):
            a, c = part[r][h], part[h][r]
            if h == r: a, c = a[:PAIR // 2], a[PAIR // 2:]
            back[a] = c
            back[c] = a
    return lay(back)
def setup_inputs(rng):
    return {"b": lift(f(rng, N, 128, 4 * V)), "m": lift(f(rng, N, 128, 4 * E)), "u": f(rng, N, 128, 512), "w": f(rng, N, 128, 512 * O), "rev": links(rng)}
def setup_inputs_ties(rng):
    d = setup_inputs(rng)
    x = rng.integers(4, 8, (128, 1, 4)) * np.exp2(rng.integers(-2, 1, (128, 1, 4))) * rng.choice([-1.0, 1.0], (128, 1, 4))
    double = rng.permutation(N) < N // 2
    d["b"] = np.stack([np.repeat(x * (1 + double[r]), V, axis=1).reshape(128, 4 * V) for r in range(N)]).astype(np.float32).astype(BF)
    d["m"] = np.stack([np.repeat(x, E, axis=1).reshape(128, 4 * E) for r in range(N)]).astype(np.float32).astype(BF)
    return d
def setup_inputs_near(rng):
    d = setup_inputs(rng)
    p = 8 * rng.permutation(16)[:3] + rng.integers(0, 8, 3)
    t = rng.integers(0, 4, 3)
    i = np.arange(V)
    rows = [np.full(V, 32), 4 * (i % 8), 4 * (i // 8)]
    g = 1.0 - 2 * rng.integers(0, 2, N)
    b, m, u = np.array(d["b"]).reshape(N, 128, V, 4), np.array(d["m"]).reshape(N, 128, E, 4), np.array(d["u"])
    u[:, :, :4] = 0
    for k in range(3):
        b[:, p[k], :, t[k]] = np.broadcast_to(rows[k], (N, V)).astype(np.float32).astype(BF)
        m[:, p[k], :, t[k]] = 0
        u[:, p[k], t[k]] = (g * 2.0 ** (0, -19, -16)[k]).astype(np.float32).astype(BF)
    d["b"], d["m"], d["u"] = b.reshape(N, 128, 4 * V), m.reshape(N, 128, 4 * E), u
    return d
def setup_inputs_huge_order(rng):
    d = setup_inputs(rng)
    for k, n in (("b", V), ("m", E)):
        sign = np.repeat(1 - 2 * rng.integers(0, 2, (N, 1, n)), 4, axis=2)
        d[k] = ((1 + rng.random((N, 128, 4 * n))) * 2.0 ** 27 * sign).astype(np.float32).astype(BF)
    u = np.array(d["u"])
    u[:, :, :4] = ((1 + rng.random((N, 128, 4))) * 2.0 ** 29 * (1 - 2 * rng.integers(0, 2, (N, 1, 1)))).astype(np.float32).astype(BF)
    d["u"] = u
    for g in rng.permutation(16)[:2]:
        x = rng.integers(4, 8, (8, 1, 4)) * 2.0 ** 25 * rng.choice([-1.0, 1.0], (8, 1, 4))
        kind = rng.integers(-1, 2, (N, 1, E, 1))
        small = rng.integers(1, 8, (N, 8, E, 4)) * 0.25 * rng.choice([-1.0, 1.0], (N, 8, E, 4))
        nodes = x * (1 - 2 * rng.integers(0, 2, (N, 1, V, 1)))
        d["b"][:, 8 * g:8 * g + 8] = nodes.reshape(N, 8, 4 * V).astype(np.float32).astype(BF)
        d["m"][:, 8 * g:8 * g + 8] = np.where(kind == 0, small, x * kind).reshape(N, 8, 4 * E).astype(np.float32).astype(BF)
    return d
def setup_inputs_blocks(rng):
    d = setup_inputs(rng)
    spots = [np.arange(V).reshape(N, PAIR // 4)[rng.permutation(N)] + V * r for r in range(N)]
    back, keep, four = np.zeros(N * E, int), np.zeros(N * V, bool), np.arange(4)
    for r in range(N):
        for h in range(r, N):
            a, c = spots[r][h], rng.permutation(spots[h][r])
            if h == r: c = a
            for k in range(PAIR // 4):
                q = rng.permutation(4)
                if h == r:
                    back[4 * a[k] + q] = 4 * a[k] + q[[1, 0, 3, 2]]
                else:
                    back[4 * a[k] + four] = 4 * c[k] + q
                    back[4 * c[k] + q] = 4 * a[k] + four
            on = rng.integers(0, PAIR // 4)
            if (r + h) % 2 == 0:
                keep[a[on]] = True
                keep[c[on]] = True
            else:
                keep[a] = True
                keep[c] = True
    d["b"] = np.where(np.repeat(keep.reshape(N, 1, V), 4, axis=2), d["b"], np.zeros_like(d["b"]))
    d["m"] = np.where(np.repeat(keep.reshape(N, 1, V), 16, axis=2), d["m"], np.zeros_like(d["m"]))
    d["rev"] = lay(back)
    return d
def setup_inputs_spread(rng):
    d = {**setup_inputs(rng), "b": lift(wide(rng, N, 128, 4 * V, cols=6)), "m": lift(wide(rng, N, 128, 4 * E, cols=6))}
    u = np.array(d["u"])
    u[int(rng.integers(0, N)), :, :4] = 0
    return {**d, "u": u}
def check_inputs(d):
    bad = []
    for k, low, high in (("b", -12, 28), ("m", -12, 28), ("u", -30, 30), ("w", -30, 30)):
        v = np.abs(d[k].astype(np.float32))
        if not (np.isfinite(v).all() and ((v == 0) | (v >= 2.0 ** low) & (v <= 2.0 ** high)).all()): bad.append("a value of " + k)
    back = np.concatenate([entries(d["rev"][r]) for r in range(N)])
    if back.min() < 0 or back.max() >= N * E:
        bad.append("rev is out of range")
        return bad
    e = np.arange(N * E)
    if (back[back] != e).any() or (back == e).any(): bad.append("rev isn't made of pairs of different edges")
    if (np.bincount(e // E * N + back // E, minlength=N * N) != PAIR).any(): bad.append("edges of a pair of ranks")
    return bad
def reference(b, m, u, w, rev):
    y, up = np.zeros((N, 128, R * O * E), np.float32), np.zeros((N, 1, E), np.float32)
    oc, osc = np.zeros((N, 128, 4 * E), np.uint8), np.zeros((N, 16, E), np.uint8)
    back = np.concatenate([entries(rev[r]) for r in range(N)])
    e = np.arange(N * E)
    head = back // E
    others = np.array([[k for k in range(4) if k != j] for j in range(4)])
    come = back[4 * (e // 4)[:, None] + others[e % 4]]
    msg = mx_ref.quantize(np.concatenate([m[r] for r in range(N)], axis=1))
    dm = decode(msg).reshape(128, N * E, 4)
    db = decode(mx_ref.quantize(np.concatenate([b[r] for r in range(N)], axis=1))).reshape(128, N * V, 4)
    qu = [mx_ref.quantize(np.ascontiguousarray(u[r])) for r in range(N)]
    qw = [[mx_ref.quantize(np.ascontiguousarray(cut(w[r], o))) for o in range(O)] for r in range(N)]
    for t in range(R):
        z = db[:, e // 4]
        for j in range(3): z = z + dm[:, come[:, j]]
        z = z * np.float32(0.25)
        cand = mx_ref.quantize(np.ascontiguousarray(z.reshape(128, -1).astype(BF)))
        dc = decode(cand).reshape(128, N * E, 4)
        change = mx_ref.quantize(np.ascontiguousarray((dc - dm).reshape(128, -1).astype(BF)))
        taken = []
        for r in range(N):
            s = np.abs(mx_ref.matmul(qu[r], pick(change, np.arange(E * r, E * r + E)))[0]) + np.float32(0)
            for h in range(N):
                k = np.flatnonzero(head[E * r:E * r + E] == h)
                k = k[np.argsort(-s[k], kind="stable")[:CAP]]
                up[r, 0, k] += 1
                taken.append(E * r + k)
        taken = np.concatenate(taken)
        msg = put(msg, taken, pick(cand, taken))
        dm[:, taken] = dc[:, taken]
        for r in range(N):
            new = np.arange(E * r, E * r + E) if t == 0 else taken[N * CAP * r:N * CAP * r + N * CAP]
            now = pick(msg, new)
            for o in range(O):
                i = (t * O + o) * E
                if t > 0: y[r, :, i:i + E] = y[r, :, i - O * E:i - O * E + E]
                y[r][:, i + new - E * r] = mx_ref.matmul(qw[r][o], now)
    for r in range(N): oc[r], osc[r] = emit(pick(msg, np.arange(E * r, E * r + E)))
    return {"y": y, "oc": oc, "osc": osc, "up": up}

@@ -1,0 +1,583 @@
+from concourse.bass import DstId, RemoteDMATransfer
+from concourse.mybir import dt, AluOpType as A, AxisListType, ActivationFunctionType as F
+
+N, V, E, R, O, K = 8, 32, 128, 3, 2, 16
+X4, U8, U16, BF, F32, I32 = "float8_e4m3fn_x4", "uint8", "uint16", "bfloat16", "float32", "int32"
+EPS = 2.0 ** -120
+BIG = 1.5 * 2.0 ** 30
+SCRATCH = {}
+
+
+def _buf(name, cols, dtype, where="sbuf"):
+    SCRATCH[name] = (where, [128, cols], dtype)
+
+
+for _i in range(4):
+    _buf("zb%d" % _i, 512, F32, "psum")
+    _buf("db%d" % _i, 512, F32, "psum")
+for _n, _c, _d in (
+        ("wr", 10, I32), ("mb", 768, BF), ("uc", 4, BF), ("wt", 1024, BF), ("pw", 512, BF),
+        ("one", 128, BF), ("ij", 128, BF), ("eb", 516, BF), ("nb", 516, BF), ("pb", 512, BF), ("gb", 512, BF), ("ub", 512, BF), ("pk", 512, BF), ("pn", 512, BF),
+        ("im16", 128, BF), ("pa", 128, F32), ("t1", 64, F32), ("c32", 32, F32), ("k24", 24, F32),
+        ("ki", 10, I32), ("ku", 10, U16), ("kf", 12, F32), ("cf", 112, F32), ("hx", 34, F32), ("lff", 24, F32), ("sm", 8, F32), ("tt", 48, F32),
+        ("li", 32, I32), ("ld", 32, I32), ("l4", 32, I32), ("fw", 72, F32), ("ls", 16, U16), ("fd", 24, U16), ("lf", 24, U16), ("ln", 16, U16),
+        ("ah", 128, BF), ("mk", 128, BF), ("cu", 128, BF), ("jk", 136, BF),
+        ("ar", 128, F32), ("rb", 128, F32), ("js", 512, BF), ("asl", 128, BF), ("slb", 128, BF), ("dk", 384, BF), ("dkt", 384, BF),
+        ("eq", 16, I32), ("ei", 2, I32), ("ef", 4, F32), ("oh", 16, F32), ("hk", 256, BF),
+        ("yv0", 128, F32), ("yv1", 128, F32), ("yw0", 256, F32), ("yw1", 256, F32), ("ups", 128, F32),
+        ("z", 512, BF), ("dd", 512, BF), ("sx", 128, F32)):
+    _buf(_n, _c, _d)
+for _n, _c in (("qmb", 160), ("qx", 128), ("qp", 128), ("bb", 128), ("ep", 512), ("en", 512), ("pc", 128), ("qg", 128), ("qk", 128), ("qn", 128), ("qu", 128), ("qw", 256), ("qd", 128),
+               ("mw0", 256), ("mw1", 256), ("mw2", 256), ("iw0", 256), ("iw1", 256), ("iw2", 128),
+               ("rm0", 32), ("rc0", 64), ("rc1", 64), ("f0", 384), ("f1", 384), ("f2", 384), ("nt", 128)):
+    _buf(_n, _c, X4)
+    _buf(_n + "_s", _c, U8)
+for _t in range(R):
+    _buf("ys%d" % _t, 256, F32)
+for _t in range(R - 1):
+    _buf("lst%d" % _t, 16, U16)
+    _buf("rl%d" % _t, 8, U16)
+    _buf("rq%d" % _t, 2, U16)
+
+STAGES = ["m0", "m0s", "c0", "c0s", "l0", "c1", "c1s", "l1"]
+SEMAPHORES = ["qv", "qs", "qt", "qg", "ls", "lf", "ldr", "ldm", "ldu", "ldw", "hm0", "hc0", "hc1", "hl0", "hl1", "st", "b_l0", "b_l1"]
+SEMAPHORES += ["a_" + s for s in STAGES] + ["r_" + s for s in STAGES]
+FAR, NEAR = 0, 1
+
+
+def direct(T, topo, c):
+    return [d for d in T.cores if d != c and topo.may_write(c, d)]
+
+
+def cross(T, topo, c):
+    return [d for d in T.cores if d != c and not topo.may_write(c, d)]
+
+
+def peers(T, topo, c):
+    return [x for x in topo.cores_of(c) if T.rank_of(x) is not None]
+
+
+def relay(T, topo, c, d):
+    own = [x for x in topo.cores_of(c) if T.rank_of(x) is None and topo.may_write(x, d)]
+    near = [x for x in own if topo.die(x) == topo.die(d)] or own
+    same = [x for x in cross(T, topo, c) if topo.die(x) == topo.die(d)]
+    return near[same.index(d) % len(near)]
+
+
+def chips(T, topo, c):
+    out = []
+    for d in cross(T, topo, c):
+        if not out or d not in topo.cores_of(out[-1][0]):
+            out.append([])
+        out[-1].append(d)
+    return out
+
+
+def runs(T, topo, c):
+    out = []
+    for r, d in enumerate(T.cores):
+        way = NEAR if d == c or topo.may_write(d, c) else FAR
+        if out and out[-1][2] == way:
+            out[-1][1] += 1
+        else:
+            out.append([r, 1, way])
+    if any(r % 2 for r, _, _ in out):
+        out = [[0, N, FAR]]
+    return out
+
+
+def pow2(n):
+    k = 1
+    while 2 * k <= n:
+        k *= 2
+    return k
+
+
+def share(topo, c, dsts):
+    off = [d for d in dsts if d not in topo.cores_of(c)]
+    on = [d for d in dsts if d in topo.cores_of(c)]
+    out = {}
+    every = topo.engines(c, on[0]) if on else topo.engines(c, off[0])
+    per = pow2(len(every) // len(dsts))
+    used = []
+    for i, d in enumerate(off):
+        out[d] = topo.engines(c, d)[per * i:per * i + per]
+        used += out[d]
+    left = [e for e in every if e not in used]
+    per = pow2(len(left) // len(on)) if on else 0
+    for i, d in enumerate(on):
+        out[d] = left[per * i:per * i + per]
+    return out
+
+
+def bits(engines):
+    return sum(1 << e for e in engines)
+
+
+def kind(stage):
+    return int(stage[1]), "_s" if stage.endswith("s") else "", stage[0] != "l" and not stage.endswith("s"), E if stage[0] == "c" else 0
+
+
+def roads(T, topo, c, stage, way):
+    if way == NEAR:
+        out = [(d, [d]) for d in direct(T, topo, c)]
+    elif stage[0] == "c":
+        out = [(relay(T, topo, c, ds[(j + stage.endswith("s")) % len(ds)]), ds) for j, ds in enumerate(chips(T, topo, c))]
+    else:
+        out = [(relay(T, topo, c, d), [d]) for d in cross(T, topo, c)]
+    e = share(topo, c, [x for x, _ in out])
+    return [(x, e[x], ds) for x, ds in out]
+
+
+def onward(T, topo, x, stage):
+    mine = peers(T, topo, x)
+    ds = [r[2] for r in roads(T, topo, mine[0], stage, FAR) if r[0] == x] if mine else []
+    if not ds:
+        return []
+    ds = ds[0]
+    if len(ds) == 1:
+        return [(ds[0], topo.engines(x, ds[0]), 0, len(mine), mine[0])]
+    e = topo.engines(x, ds[0])
+    per = pow2(len(e) // (len(mine) * len(ds)))
+    out = []
+    for i, s in enumerate(mine):
+        for j, d in enumerate(ds):
+            k = len(out)
+            out.append((d, e[per * k:per * k + per], i * len(ds) + j, 1, s))
+    return out
+
+
+def arrival(stage, way):
+    return ("b_" if stage[0] == "l" and way == FAR else "a_") + stage
+
+
+def landed(T, topo, c, stage):
+    n = {}
+    rank = T.rank_of(c) is not None
+    for s in T.cores:
+        if s != c:
+            for way in (FAR, NEAR):
+                k = arrival(stage, way) if rank else "r_" + stage
+                n[k] = n.get(k, 0) + sum(len(e) for x, e, _ in roads(T, topo, s, stage, way) if x == c)
+        if rank and s == peers(T, topo, s)[0] and not topo.may_write(s, c):
+            k = arrival(stage, FAR)
+            n[k] = n.get(k, 0) + sum(len(o[1]) for x in topo.cores_of(s) if T.rank_of(x) is None for o in onward(T, topo, x, stage) if o[0] == c)
+    return n
+
+
+def view(T, name, a, n, codes):
+    x = T[name][:, a:a + n]
+    return x.bitcast(dt.uint8) if codes else x
+
+
+def relay_program(g, core, T, topo):
+    total = 0
+    for st in STAGES:
+        out = onward(T, topo, core, st)
+        if not out:
+            continue
+        t, tail, codes, base = kind(st)
+        tr = []
+        for d, e, a, n, s in out:
+            r = T.rank_of(s)
+            if st[0] == "l":
+                src, dst = T["rq%d" % t][:, a:a + n], T["rl%d" % t][:, r:r + n]
+            else:
+                src, dst = view(T, "r" + st[:2] + tail, K * a, K * n, codes), view(T, "iw%d" % t + tail, base + K * r, K * n, codes)
+            rid, pid = topo.addr(d, core)
+            tr.append(RemoteDMATransfer(dst_ids=[DstId(rid=rid, pnc=pid)], dma_engine_mask=bits(e), remote_sem=T.sem[arrival(st, FAR)], src=src, dst=dst))
+            total += len(e)
+        g.wait_ge(T.sem["r_" + st], landed(T, topo, core, st)["r_" + st])
+        g.remote_dma_fused(tr, local_sem=T.sem["ls"])
+    if total:
+        g.wait_ge(T.sem["ls"], total)
+
+
+def rank_program(g, core, T, topo):
+    rank = T.rank_of(core)
+    if rank is None:
+        if peers(T, topo, core):
+            relay_program(g, core, T, topo)
+        return
+    q = {"v": g.vector, "s": g.scalar, "t": g.tensor, "g": g, "y": g.sync}
+    count, seen, wrote, read, want = {}, {}, {}, {}, {}
+
+    def need(k, toks):
+        for s, n in toks:
+            if not (k == "t" and s == "qt") and seen.get((k, s), 0) < n:
+                want[s] = max(want.get(s, 0), n)
+
+    def waits(k, rd, wr):
+        want.clear()
+        for r in rd:
+            need(k, wrote.get(r, []))
+        for w in wr:
+            need(k, wrote.get(w, []))
+            need(k, read.get(w, []))
+        for s, n in want.items():
+            q[k].wait_ge(T.sem[s], n)
+            seen[(k, s)] = n
+
+    def note(tok, rd, wr):
+        for r in rd:
+            read.setdefault(r, []).append(tok)
+        for w in wr:
+            wrote[w] = [tok]
+            read[w] = []
+
+    def op(k, fn, rd=(), wr=()):
+        waits(k, rd, wr)
+        s = "q" + k
+        fn().then_inc(T.sem[s], 1)
+        count[s] = count.get(s, 0) + 1
+        note((s, count[s]), rd, wr)
+
+    def dmas(parts, s, rd=(), wr=()):
+        for k in sorted({p[0] for p in parts}):
+            waits(k, rd, wr)
+        for k, o, i in parts:
+            q[k].dma_start(o, i).then_inc(T.sem[s], 16)
+            count[s] = count.get(s, 0) + 16
+        note((s, count[s]), rd, wr)
+
+    v, sc, te = g.vector, g.scalar, g.tensor
+    u32 = dt.uint32
+
+    def tsc(o, i, s1, s2, o1, o2, rd, wr):
+        if o2 is None:
+            op("v", lambda: v.tensor_scalar(o, i, s1, None, o1), rd, wr)
+        else:
+            op("v", lambda: v.tensor_scalar(o, i, s1, s2, o1, o2), rd, wr)
+
+    def cp(o, i, rd, wr):
+        op("v", lambda: v.tensor_copy(o, i), rd, wr)
+
+    def ttn(o, a, b, f, rd, wr):
+        op("v", lambda: v.tensor_tensor(o, a, b, f), rd, wr)
+
+    def fill(o, x, rd, wr):
+        op("v", lambda: v.memset(o, x), rd, wr)
+
+    def turn(o, i, rd, wr):
+        op("v", lambda: v.transpose(o, i), rd, wr)
+
+    def act(o, i, fn, rd, wr, **kw):
+        op("s", lambda: sc.activation(o, i, fn, **kw), rd, wr)
+
+    def iota(o, pattern, ch, wr, base=0):
+        op("g", lambda: g.iota(o, pattern, base, ch, allow_small_or_imprecise_dtypes=True), (), [wr])
+
+    def quant(name, a, b, tile, x, rd, wr):
+        op("v", lambda: v.quantize_mx(T[name][:, a:b], T[name + "_s"][:, a:b], T[tile][:, x:x + 4 * (b - a)]), rd, wr)
+
+    def pick(out, a, n, src, c, d, off, e, codes, scales, lists, wc, ws):
+        op("v", lambda: v.tensor_copy(T[out][:, a:a + n].bitcast(u32), T[src][:, c:d].bitcast(u32).indirect(T[off][:, e:e + n // K])), codes + lists, [wc])
+        op("s", lambda: sc.activation(T[out + "_s"][:, a:a + n], T[src + "_s"][:, c:d].indirect(T[off][:, e:e + n // K]), F.Copy), scales + lists, [ws])
+
+    def mm(bank, ln, la, rn, ra, start, stop, rd):
+        op("t", lambda: te.matmul_mx(T[bank][:, 0:128], T[ln][:, la:la + 128], T[ln + "_s"][:, la:la + 128],
+                                     T[rn][:, ra:ra + 128], T[rn + "_s"][:, ra:ra + 128], start, stop), rd, [bank])
+
+    parts = []
+    for a in range(4):
+        for d in range(2):
+            parts.append(("ys"[d], T.wr[32 * a + 16 * d:32 * a + 16 * d + 16, 1 - d:9 - d], T.rev[:, :]))
+    dmas(parts, "ldr", (), ["wr"])
+    dmas([("y", T.mb[:, 0:512], T.m[:, :]), ("s", T.mb[:, 512:640], T.b[:, :])], "ldm", (), ["mb"])
+    dmas([("y", T.uc[:, :], T.u[:, 0:4])], "ldu", (), ["uc"])
+    dmas([("y", T.wt[:, :], T.w[:, :])], "ldw", (), ["wt"])
+
+    op("g", lambda: g.iota(T.ki[:, 0:2], [[0, 2]], 0, 1), (), ["ip"])
+    iota(T.im16[:, :], [[0, 8], [1, 16]], 0, "im16")
+    iota(T.t1[:, 32:64], [[128, 2], [0, 16]], 0, "tq")
+    iota(T.ij[:, :], [[1, 128]], 0, "ij")
+    iota(T.c32[:, :], [[1, 2], [1, 16]], 0, "c32")
+    iota(T.mb[:, 640:768], [[0, 128]], 0, "xz")
+    iota(T.cf[:, 0:16], [[0, 2], [1, 8]], 0, "c8")
+    iota(T.k24[:, :], [[1, 3], [0, 8]], 0, "k24")
+    fill(T.eb[:, :], 0.0, (), ["ebz"])
+    fill(T.one[:, :], 1.0, (), ["one"])
+    tsc(T.ki[:, 2:4], T.ki[:, 0:2], 15, None, A.bitwise_and, None, ["ip"], ["i2"])
+    tsc(T.ki[:, 4:6], T.ki[:, 0:2], 4, None, A.logical_shift_right, None, ["ip"], ["i4"])
+    tsc(T.ki[:, 6:8], T.ki[:, 0:2], 22, None, A.bitwise_and, None, ["ip"], ["i6"])
+    tsc(T.ki[:, 8:10], T.ki[:, 0:2], 5, None, A.logical_shift_right, None, ["ip"], ["i8"])
+    cp(T.kf[:, 0:10], T.ki[:, :], ["ip", "i2", "i4", "i6", "i8"], ["kf"])
+    tsc(T.kf[:, 11:12], T.ki[:, 8:9], 256.0, BIG, A.mult, A.add, ["i8"], ["kc"])
+    tsc(T.t1[:, 0:32], T.t1[:, 32:64], T.kf[:, 11:12], None, A.add, None, ["tq", "kc"], ["t1"])
+    tsc(T.kf[:, 10:11], T.ki[:, 2:3], 0.5, None, A.add, None, ["i2"], ["kh"])
+    cp(T.ku[:, :], T.ki[:, :], ["ip", "i2", "i4", "i6", "i8"], ["ku"])
+    p1, k16, g16, k05 = T.kf[:, 0:1], T.kf[:, 2:3], T.kf[:, 4:5], T.kf[:, 10:11]
+    act(T.pa[:, :], T.im16[:, :], F.Abs, ["im16", "kf"], ["pa"], scale=-1.0, bias=k16)
+    for i, c in enumerate((0.5, 8.0, 0.5, 0.5)):
+        act(T.pw[:, i:512:4], T.pa[:, :], F.Relu, ["pa"], ["pw%d" % i], scale=-c, bias=c)
+
+    def spread(dst, col, rd, both):
+        for b in range(4):
+            o, x = T[dst][:, 32 * b:32 * b + 32], T.lff[:, col + b:col + b + 1]
+            if both and b % 2:
+                tsc(o, T.one[:, 0:32], x, None, A.mult, None, ["one", rd], [dst + ".%d" % b])
+            else:
+                act(o, T.one[:, 0:32], F.Copy, ["one", rd], [dst + ".%d" % b], scale=x)
+
+    tsc(T.lff[:, 0:4], T.wr[:, 1:9:2], 63.75, BIG, A.subtract, A.add, ["wr"], ["h4"])
+    for b in range(4):
+        tsc(T.ah[:, 32 * b:32 * b + 32], T.t1[:, 0:32], T.lff[:, b:b + 1], None, A.is_equal, None, ["t1", "h4"], ["ah%d" % b])
+    turn(T.mk[:, :], T.ah[:, :], ["ah%d" % b for b in range(4)], ["mk"])
+    op("v", lambda: v.tensor_tensor_scan(T.cu[:, :], T.mk[:, :], T.mk[:, :], 0.0, A.add, A.max), ["mk"], ["cu"])
+    act(T.jk[:, 128:136], T.cu[:, 15:128:16], F.Sign, ["cu", "kh"], ["jb", "acc1"], scale=-1.0, bias=k05, accum_out=T.lff[:, 17:18])
+    act(T.jk[:, 0:128], T.cu[:, :], F.Sign, ["cu", "kh"], ["jk", "acc0"], scale=-1.0, bias=k05, accum_out=T.lff[:, 16:17])
+    cp(T.lff[:, 4:8], T.wr[:, 1:9:2], ["wr"], ["r4f"])
+    quant("qp", 0, 128, "pw", 0, ["pw%d" % i for i in range(4)], ["qp"])
+    tsc(T.mb[:, 641:768:4], T.c32[:, :], g16, T.lff[:, 17:18], A.is_equal, A.mult, ["c32", "kf", "acc1", "xz"], ["x1"])
+    tsc(T.lff[:, 18:19], T.lff[:, 17:18], -16.0, T.lff[:, 16:17], A.mult, A.add, ["acc0", "acc1"], ["low"])
+    tsc(T.mb[:, 640:768:4], T.c32[:, :], g16, T.lff[:, 18:19], A.is_equal, A.mult, ["c32", "kf", "low", "xz"], ["x0"])
+    quant("qx", 0, 128, "mb", 256, ["mb", "xz", "x0", "x1"], ["qx"])
+    mm("db0", "qp", 0, "qx", 0, True, True, ["qp", "qx"])
+    quant("qmb", 0, 160, "mb", 0, ["mb"], ["qmb"])
+    spread("ar", 4, "r4f", False)
+    act(T.cf[:, 48:64], T.im16[:, 0:16], F.Relu, ["im16", "kf"], ["below"], scale=-1.0, bias=k16)
+    act(T.cf[:, 96:112], T.cf[:, 0:16], F.Abs, ["c8", "kf"], ["away"], scale=-1.0, bias=g16)
+    act(T.cf[:, 80:96], T.cf[:, 48:64], F.Sign, ["below"], ["lt"])
+    act(T.hx[:, 0:16], T.cf[:, 96:112], F.Relu, ["away"], ["hm"], scale=-8.0, bias=8.0)
+    act(T.cf[:, 64:80], T.cf[:, 80:96], F.Copy, ["lt"], ["mth"], scale=-2.0 ** -24, bias=1.0)
+    act(T.lff[:, 20:24], T.uc[:, :], F.Copy, ["uc"], ["ucf"])
+    tsc(T.ls[:, 0:8], T.db0[:, 96:104], 64.0, None, A.add, None, ["db0"], ["ls"])
+    pick("mw0", 0, 128, "qmb", 0, 128, "ls", 0, ["qmb"], ["qmb"], ["ls"], "mw0.m", "mw0.m_s")
+
+    def send(stage, way, src, rd, local="ls"):
+        t, tail, codes, base = kind(stage)
+        i = peers(T, topo, core).index(core)
+        waits("g", rd, ())
+        tr = []
+        for x, e, ds in roads(T, topo, core, stage, way):
+            n = len(ds)
+            if stage[0] == "l":
+                dst = T["rl%d" % t][:, rank:rank + 1] if way == NEAR else T["rq%d" % t][:, i:i + 1]
+            elif way == NEAR:
+                dst = view(T, "iw%d" % t + tail, base + K * rank, K, codes)
+            else:
+                dst = view(T, "r" + stage[:2] + tail, K * n * i, K * n, codes)
+            rid, pid = topo.addr(x, core)
+            tr.append(RemoteDMATransfer(dst_ids=[DstId(rid=rid, pnc=pid)], dma_engine_mask=bits(e),
+                                        remote_sem=T.sem[arrival(stage, NEAR) if way == NEAR else "r_" + stage], src=src(T.rank_of(ds[0]), n), dst=dst))
+            count[local] = count.get(local, 0) + len(e)
+        g.remote_dma_fused(tr, local_sem=T.sem[local])
+        count.update(landed(T, topo, core, stage))
+
+    def columns(stage, way, local="ls"):
+        t, tail, codes, base = kind(stage)
+        m = "mw%d" % t
+        send(stage, way, lambda h, n: view(T, m + tail, base + K * h, K * n, codes), [m + (".c" if base else ".m") + tail], local)
+
+    def home(stage, after):
+        t, _, _, base = kind(stage)
+        m, iw, part, at = "mw%d" % t, "iw%d" % t, ".c" if base else ".m", base + K * rank
+        dmas([("y", view(T, iw, at, K, True), view(T, m, at, K, True)),
+              ("y", view(T, iw + "_s", at, K, False), view(T, m + "_s", at, K, False))], "h" + stage, [m + part, m + part + "_s"] + after, ["home"])
+        h = wrote.pop("home")
+        for x, y in (("", ""), ("s", "_s")):
+            wrote[iw + part + y] = [("a_" + stage + x, count["a_" + stage + x])] + h
+
+    for way, local in ((FAR, "lf"), (NEAR, "ls")):
+        for st in ("m0", "m0s"):
+            columns(st, way, local)
+    wrote["left"] = [("lf", count["lf"])]
+    home("m0", ["left"])
+    iota(T.pb[:, :], [[0, 512]], 0, "pb", 1)
+    iota(T.nb[:, :], [[0, 516]], 0, "nbz")
+    iota(T.gb[:, :], [[0, 512]], 0, "gb")
+    iota(T.cf[:, 16:32], [[16, 8], [0, 2]], 0, "h16")
+
+    turn(T.rb[:, :], T.ar[:, :], ["ar.%d" % b for b in range(4)], ["rb"])
+    for b in range(4):
+        act(T.js[:, 128 * b:128 * b + 128], T.rb[:, :], F.Sign, ["rb", "r4f"], ["js%d" % b, "sa%d" % b], scale=-1.0, bias=T.lff[:, 4 + b:5 + b], accum_out=T.lff[:, 8 + b:9 + b])
+    tsc(T.li[:, :], T.db0[:, 96:128], 64.0, None, A.add, None, ["db0"], ["li"])
+    cp(T.ld[:, :], T.li[:, :].indirect(T.ku[:, 6:8]), ["li", "ku"], ["ld"])
+    tsc(T.l4[:, 24:32], T.li[:, 0:8], 2, None, A.logical_shift_right, None, ["li"], ["l2"])
+    tsc(T.l4[:, 0:24], T.ld[:, 0:24], 124, None, A.bitwise_and, None, ["ld"], ["l4"])
+    cp(T.ls[:, 8:16], T.l4[:, 24:32], ["l2"], ["lb"])
+    ttn(T.fw[:, 0:24], T.l4[:, 0:24], T.k24[:, :], A.add, ["l4", "k24"], ["fw"])
+    ttn(T.fw[:, 24:48], T.fw[:, 0:24], T.ld[:, 0:24], A.is_ge, ["fw", "ld"], ["fc"])
+    ttn(T.fw[:, 48:72], T.fw[:, 0:24], T.fw[:, 24:48], A.add, ["fw", "fc"], ["fk"])
+    cp(T.fd[:, :], T.fw[:, 48:72], ["fk"], ["fd"])
+    pick("bb", 0, 128, "qmb", 128, 160, "ls", 8, ["qmb"], ["qmb"], ["lb"], "bb", "bb_s")
+    tsc(T.lff[:, 12:16], T.lff[:, 8:12], 0.5, 63.5, A.mult, A.add, ["sa%d" % b for b in range(4)], ["s4"])
+    spread("asl", 12, "s4", True)
+    tsc(T.eb[:, 3:512:4], T.ij[:, :], p1, None, A.is_equal, None, ["ij", "kf", "ebz"], ["ebh"])
+    turn(T.slb[:, :], T.asl[:, :], ["asl.%d" % b for b in range(4)], ["slb"])
+    cp(T.dk[:, 0:192], T.slb[:, :].indirect(T.fd[:, 0:12]), ["slb", "fd"], ["dk0"])
+    act(T.dk[:, 192:384], T.slb[:, :].indirect(T.fd[:, 12:24]), F.Copy, ["slb", "fd"], ["dk1"])
+
+    def unpacking(b):
+        quant("ep", 128 * b, 128 * b + 128, "eb", 3 - b, ["ebz", "ebh"], ["ep%d" % b])
+
+    for b in (0, 1):
+        unpacking(b)
+    turn(T.dkt[:, :], T.dk[:, :], ["dk0", "dk1"], ["dkt"])
+    cp(T.lf[:, :], T.dkt[:, 0:384:16], ["dkt"], ["lf"])
+    for b in (2, 3):
+        unpacking(b)
+    act(T.pb[:, 0:512:4], T.pa[:, :], F.Relu, ["pa", "pb"], ["pb0"], scale=-128.0, bias=128.0)
+    act(T.pb[:, 2:512:4], T.im16[:, :], F.Copy, ["im16", "pb"], ["pb2"])
+
+    def tile_u(t):
+        act(T.ub[:, t:512:4], T.one[:, :], F.Copy, ["one", "ucf"], ["ub%d" % t], scale=T.lff[:, 20 + t:21 + t])
+
+    for b in (0, 1):
+        tile_u(b)
+
+    def prefill_m(t):
+        for b in range(4):
+            mm("db%d" % b, "en", 128 * b, "mw%d" % t, 0, True, False, ["en%d" % b, "mw%d.m" % t, "mw%d.m_s" % t])
+
+    def prefill_b():
+        for b in range(4):
+            mm("zb%d" % b, "ep", 128 * b, "bb", 0, True, False, ["ep%d" % b, "bb", "bb_s"])
+
+    prefill_b()
+    seg = runs(T, topo, core)
+    flags = ["gb", "gb0", "gb1", "gb3", "gb4", "gb5", "gb6", "gb7"]
+
+    def inw(t, tail):
+        return ["iw%d.m%s" % (t, tail)] if t == 0 else ["iw%d.m%s.%d" % (t, tail, r) for r, _, _ in seg]
+
+    def results(i, src, m):
+        act(T["ys%d" % i][:, 0:128], T[src + "0"][:, 0:128].indirect(T.ln[:, 0:8]), F.Copy, [src + "0" + m, "ln"], ["ys%d.0" % i])
+        cp(T["ys%d" % i][:, 128:256], T[src + "1"][:, 0:128].indirect(T.ln[:, 0:8]), [src + "1" + m, "ln"], ["ys%d.1" % i])
+        dmas([("y", T.y[:, 256 * i:256 * i + 256], T["ys%d" % i][:, :])], "st", ["ys%d.0" % i, "ys%d.1" % i], ())
+
+    for t in range(R):
+        iw, mw, f = "iw%d" % t, "mw%d" % t, "f%d" % t
+        nw, last = "mw%d" % (t + 1), t == R - 1
+        for k in range(3):
+            pick(f, 128 * k, 128, iw, 0, 128, "lf", 8 * k, inw(t, ""), inw(t, "_s"), ["lf"], f + ".%d" % k, f + "s.%d" % k)
+        for k in range(3):
+            for b in range(4):
+                mm("zb%d" % b, "ep", 128 * b, f, 128 * k, False, k == 2, ["ep%d" % b, f + ".%d" % k, f + "s.%d" % k])
+        if t == 0:
+            tsc(T.nb[:, 3:512:4], T.ij[:, :], p1, -1.0, A.is_equal, A.mult, ["ij", "kf", "nbz"], ["nbh"])
+            for b in range(4):
+                quant("en", 128 * b, 128 * b + 128, "nb", 3 - b, ["nbz", "nbh"], ["en%d" % b])
+            prefill_m(0)
+            for b in (2, 3):
+                tile_u(b)
+            act(T.ub[:, 4:8], T.uc[:, :], F.Copy, ["uc"] + ["ub%d" % b for b in range(4)], ["ubn"], scale=-1.0)
+        if t == 1:
+            quant("qk", 0, 128, "pk", 0, ["pk%d" % i for i in range(4)], ["qk"])
+            quant("qw", 0, 256, "wt", 0, ["wt"], ["qw"])
+        if last:
+            quant("qn", 0, 128, "pn", 0, ["pnz", "pn0", "pn3"], ["qn"])
+            results(1, "yw", ".m")
+        for b in range(4):
+            if b % 2:
+                tsc(T.z[:, b:512:4], T["zb%d" % b][:, 0:128], 0.25, None, A.mult, None, ["zb%d" % b], ["z%d" % b])
+            else:
+                act(T.z[:, b:512:4], T["zb%d" % b][:, 0:128], F.Copy, ["zb%d" % b], ["z%d" % b], scale=0.25)
+        quant(mw, 128, 256, "z", 0, ["z%d" % b for b in range(4)], [mw + ".c", mw + ".c_s"])
+        for b in range(4):
+            mm("db%d" % b, "ep", 128 * b, mw, 128, False, True, ["ep%d" % b, mw + ".c"])
+        if t == 0:
+            quant("qu", 0, 128, "ub", 0, ["ubn"] + ["ub%d" % b for b in range(4)], ["qu"])
+            quant("pc", 0, 128, "pb", 0, ["pb", "pb0", "pb2"], ["pc"])
+            act(T.gb[0:1, 1:32:4], T.one[0:1, 0:8], F.Copy, ["one", "gb"], ["gb1"], scale=float(K * rank))
+            act(T.gb[0:1, 33:64:4], T.cf[0:1, 16:32:2], F.Copy, ["h16", "gb"], ["gb3"])
+            act(T.gb[0:1, 2:64:4], T.one[0:1, 0:16], F.Copy, ["one", "gb"], ["gb4"])
+        if not last:
+            for way in (FAR, NEAR):
+                for x in ("c%d", "c%ds"):
+                    columns(x % t, way)
+        for b in range(4):
+            if b % 2:
+                cp(T.dd[:, b:512:4], T["db%d" % b][:, 0:128], ["db%d" % b], ["dd%d" % b])
+            else:
+                act(T.dd[:, b:512:4], T["db%d" % b][:, 0:128], F.Copy, ["db%d" % b], ["dd%d" % b])
+        quant("qd", 0, 128, "dd", 0, ["dd%d" % b for b in range(4)], ["qd"])
+        if last:
+            for o in range(O):
+                mm("zb%d" % (2 + o), "qw", 128 * o, mw, 128, True, True, ["qw", mw + ".c"])
+            cp(T.yw0[:, 128:256], T.zb2[:, 0:128], ["zb2"], ["yw0.c"])
+        mm("zb1", "qu", 0, "qd", 0, True, True, ["qu", "qd"])
+        mm("zb0", "qd", 0, "qu", 0, True, True, ["qu", "qd"])
+        act(T.sx[:, :], T.zb1[:, 0:128], F.Abs, ["zb1"], ["sx"], bias=EPS)
+        tsc(T.sm[:, 0:1], T.zb0[:, 0:1], T.zb0[:, 1:2], EPS, A.max, A.add, ["zb0"], ["sc"])
+        tsc(T.tt[:, 16:32], T.cf[:, 64:80], T.sm[:, 0:1], None, A.mult, None, ["mth", "sc"], ["th"])
+        ttn(T.tt[:, 32:48], T.sx[:, :].indirect(T.ku[:, 0:1]), T.tt[:, 16:32], A.is_gt, ["sx", "ku", "th"], ["kk"])
+        op("v", lambda: v.tensor_reduce(T.sm[:, 2:3], T.tt[:, 32:48], AxisListType.X, A.add), ["kk"], ["rk"])
+        if t == 0:
+            tsc(T.gb[:, 0:64:4], T.hx[:, 0:16], T.sm[:, 2:3], None, A.is_gt, None, ["hm", "rk", "gb"], ["gb0"])
+        else:
+            tsc(T.gb[:, 0:132:4], T.hx[:, 0:33], T.sm[:, 2:3], None, A.is_gt, None, ["hm", "hn", "h0", "h8", "rk", "gb"], ["gb0"])
+        quant("qg", 0, 128, "gb", 0, flags, ["qg"])
+        if last:
+            act(T.yw1[:, 128:256], T.zb3[:, 0:128], F.Copy, ["zb3"], ["yw1.c"])
+            mm("db0", "qk", 0, "qg", 0, True, True, ["qk", "qg"])
+            mm("db1", "qg", 0, "qn", 0, True, True, ["qg", "qn"])
+            cp(T.ln[:, 8:16], T.db0[:, 16:24], ["db0"], ["nl"])
+            pick("nt", 0, 128, mw, 0, 256, "ln", 8, [mw + ".m", mw + ".c"], [mw + ".m_s", mw + ".c_s"], ["nl"], "nt", "nt_s")
+            act(T.ys2[:, 0:128], T.yw0[:, :].indirect(T.ln[:, 8:16]), F.Copy, ["yw0.m", "yw0.c", "nl"], ["ys2.0"])
+            cp(T.ys2[:, 128:256], T.yw1[:, :].indirect(T.ln[:, 8:16]), ["yw1.m", "yw1.c", "nl"], ["ys2.1"])
+            cp(T.ups[:, :], T.db1[:, 0:128], ["db1"], ["ups"])
+            dmas([("y", T.oc[:, :], view(T, "nt", 0, 128, True))], "st", ["nt"], ())
+            dmas([("y", T.osc[4 * k:4 * k + 4, :], T["nt_s"][32 * k:32 * k + 4, :]) for k in range(4)], "st", ["nt_s"], ())
+            dmas([("s", T.y[:, 512:640], T.ys2[:, 0:128])], "st", ["ys2.0"], ())
+            dmas([("y", T.y[:, 640:768], T.ys2[:, 128:256])], "st", ["ys2.1"], ())
+            dmas([("s", T.up[:, :], T.ups[32:33, :])], "st", ["ups"], ())
+            break
+        lst = "lst%d" % t
+        mm("zb2", "pc", 0, "qg", 0, True, True, ["pc", "qg"])
+        if t == 0:
+            tsc(T.sm[:, 6:7], T.sm[:, 2:3], 8.0, None, A.is_lt, None, ["rk"], ["cnt"])
+        cp(T[lst][:, :], T.zb2[:, 0:16], ["zb2"], [lst])
+        for way in (FAR, NEAR):
+            send("l%d" % t, way, lambda h, n: T[lst][:, h:h + n], [lst])
+        dmas([("y", T["rl%d" % t][:, rank:rank + 1], T[lst][:, rank:rank + 1])], "hl%d" % t, [lst], ["home"])
+        h = wrote.pop("home")
+        for way in (FAR, NEAR):
+            s = arrival("l%d" % t, way)
+            wrote["rl%d.%d" % (t, way)] = [(s, count[s])] + (h if way == NEAR else [])
+        if len(seg) == 1:
+            wrote["rl%d.%d" % (t, FAR)] += wrote["rl%d.%d" % (t, NEAR)]
+        home("c%d" % t, [lst])
+        pick(nw, 0, 128, mw, 0, 256, lst, 8, [mw + ".m", mw + ".c"], [mw + ".m_s", mw + ".c_s"], [lst], nw + ".m", nw + ".m_s")
+        prefill_m(t + 1)
+        if t == 0:
+            iota(T.pn[:, :], [[0, 512]], 0, "pnz")
+            iota(T.hx[:, 24:32], [[0, 8]], 0, "h0")
+            iota(T.hx[:, 32:34], [[0, 2]], 0, "h8", 8)
+            cp(T.eq[:, :], T.li[:, :].indirect(T.ku[:, 4:5]), ["li", "ku"], ["eq"])
+            tsc(T.ei[:, 0:1], T.eq[:, 0:1], 15, None, A.bitwise_and, None, ["eq"], ["e0"])
+            tsc(T.ei[:, 1:2], T.eq[:, 0:1], 4, None, A.logical_shift_right, None, ["eq"], ["e1"])
+            cp(T.ef[:, 0:2], T.ei[:, :], ["e0", "e1"], ["ef"])
+            tsc(T.hk[:, 0:128], T.im16[:, :], T.ef[:, 0:1], None, A.is_equal, None, ["im16", "ef"], ["hk"])
+            for i, c in enumerate((128.0, 16.0, 1.0, 1.0)):
+                act(T.pk[:, i:512:4], T.hk[:, 0:128], F.Copy, ["hk"], ["pk%d" % i], scale=c)
+            cp(T.ef[:, 2:3], T.eq[:, 0:1], ["eq"], ["ee"])
+            tsc(T.hk[:, 128:256], T.ij[:, :], T.ef[:, 2:3], None, A.is_equal, None, ["ij", "ee"], ["hnn"])
+            for i in (0, 3):
+                act(T.pn[:, i:512:4], T.hk[:, 128:256], F.Copy, ["hnn", "pnz"], ["pn%d" % i])
+            tsc(T.oh[:, :], T.cf[:, 0:16], T.ef[:, 1:2], None, A.is_equal, None, ["c8", "ef"], ["oh"])
+            tsc(T.hx[:, 16:24], T.oh[:, 0:8], 8.0, None, A.mult, None, ["oh"], ["hn"])
+            tsc(T.gb[:, 65:128:4], T.oh[:, :], g16, None, A.mult, None, ["oh", "kf", "gb", "qg"], ["gb6"])
+            tsc(T.gb[:, 66:128:4], T.oh[:, :], k16, None, A.mult, None, ["oh", "kf", "gb", "qg"], ["gb7"])
+        else:
+            mm("zb3", "qk", 0, "qg", 0, True, True, ["qk", "qg"])
+            for o in range(O):
+                mm("zb%d" % o, "qw", 128 * o, mw, 0, True, True, ["qw", mw + ".m", mw + ".m_s"])
+            cp(T.ln[:, 0:8], T.zb3[:, 24:32], ["zb3"], ["ln"])
+            for o in range(O):
+                mm("zb%d" % (2 + o), "qw", 128 * o, nw, 0, True, True, ["qw", nw + ".m", nw + ".m_s"])
+            act(T.yv0[:, :], T.zb0[:, 0:128], F.Copy, ["zb0"], ["yv0"])
+            cp(T.yv1[:, :], T.zb1[:, 0:128], ["zb1"], ["yv1"])
+            act(T.yw0[:, 0:128], T.zb2[:, 0:128], F.Copy, ["zb2"], ["yw0.m"])
+            cp(T.yw1[:, 0:128], T.zb3[:, 0:128], ["zb3"], ["yw1.m"])
+            results(0, "yv", "")
+            tsc(T.gb[:, 131:132], T.sm[:, 2:3], 8.0, T.sm[:, 6:7], A.is_lt, A.add, ["rk", "cnt", "gb"], ["gb5"])
+        prefill_b()
+        ni = "iw%d" % (t + 1)
+        for way in (NEAR, FAR):
+            for r, n, w in seg:
+                if w == way:
+                    pick(ni, K * r, K * n, iw, 0, 256, "rl%d" % t, r, inw(t, "") + [iw + ".c"], inw(t, "_s") + [iw + ".c_s"],
+                         ["rl%d.%d" % (t, way)], ni + ".m.%d" % r, ni + ".m_s.%d" % r)
+    for s, n in sorted(count.items()):
+        g.wait_ge(T.sem[s], n)

@@ -16,18 +16,16 @@ for _i in range(4):
     _buf("zb%d" % _i, 512, F32, "psum")
     _buf("db%d" % _i, 512, F32, "psum")
 for _n, _c, _d in (
-        ("wr", 10, I32), ("mb", 768, BF), ("uc", 4, BF), ("wt", 1024, BF), ("pw", 512, BF),
-        ("one", 128, BF), ("ij", 128, BF), ("eb", 516, BF), ("nb", 516, BF), ("pb", 512, BF), ("gb", 512, BF), ("ub", 512, BF), ("pk", 512, BF), ("pn", 512, BF),
-        ("im16", 128, BF), ("pa", 128, F32), ("t1", 64, F32), ("c32", 32, F32), ("k24", 24, F32),
-        ("ki", 10, I32), ("ku", 10, U16), ("kf", 12, F32), ("cf", 112, F32), ("hx", 34, F32), ("lff", 24, F32), ("sm", 8, F32), ("tt", 48, F32),
-        ("li", 32, I32), ("ld", 32, I32), ("l4", 32, I32), ("fw", 72, F32), ("ls", 16, U16), ("fd", 24, U16), ("lf", 24, U16), ("ln", 16, U16),
-        ("ah", 128, BF), ("mk", 128, BF), ("cu", 128, BF), ("jk", 136, BF),
-        ("ar", 128, F32), ("rb", 128, F32), ("js", 512, BF), ("asl", 128, BF), ("slb", 128, BF), ("dk", 384, BF), ("dkt", 384, BF),
-        ("eq", 16, I32), ("ei", 2, I32), ("ef", 4, F32), ("oh", 16, F32), ("hk", 256, BF),
-        ("yv0", 128, F32), ("yv1", 128, F32), ("yw0", 256, F32), ("yw1", 256, F32), ("ups", 128, F32),
+        ("wr", 8, I32), ("rr", 128, I32), ("rb", 128, I32), ("mb", 1192, BF), ("tl", 1152, BF), ("wt", 1024, BF), ("eb", 520, BF), ("nb", 552, BF), ("tk", 512, BF),
+        ("er", 128, BF), ("im16", 128, BF), ("ij", 128, BF), ("c32", 32, F32), ("c48", 48, F32), ("k24", 24, BF), ("oh", 48, BF), ("mk", 96, BF),
+        ("ki", 12, I32), ("kf", 24, F32), ("ku", 10, U16), ("zu", 8, U16), ("ow", 6, U16), ("sg", 16, F32),
+        ("li", 16, I32), ("lif", 16, F32), ("eq", 32, F32), ("ls", 16, U16), ("lf", 24, U16), ("ln", 16, U16),
+        ("jk", 256, BF), ("ct", 128, F32), ("cm", 128, F32), ("th", 128, F32), ("kk", 16, F32), ("fl", 64, F32), ("hx", 24, F32),
+        ("yv0", 128, F32), ("yv1", 128, F32), ("yw0", 256, F32), ("yw1", 256, F32), ("ups", 2, F32),
         ("z", 512, BF), ("dd", 512, BF), ("sx", 128, F32)):
     _buf(_n, _c, _d)
-for _n, _c in (("qmb", 160), ("qx", 128), ("qp", 128), ("bb", 128), ("ep", 512), ("en", 512), ("pc", 128), ("qg", 128), ("qk", 128), ("qn", 128), ("qu", 128), ("qw", 256), ("qd", 128),
+for _n, _c in (("q1", 128), ("qa", 128), ("qmb", 160), ("qc", 152), ("qb", 128), ("q3", 152), ("bb", 128), ("ep", 512), ("en", 522), ("qr", 128), ("q0", 136), ("qg", 128),
+               ("qk", 128), ("qu", 128), ("qw", 256), ("qd", 128),
                ("mw0", 256), ("mw1", 256), ("mw2", 256), ("iw0", 256), ("iw1", 256), ("iw2", 128),
                ("rm0", 32), ("rc0", 64), ("rc1", 64), ("f0", 384), ("f1", 384), ("f2", 384), ("nt", 128)):
     _buf(_n, _c, X4)
@@ -36,11 +34,11 @@ for _t in range(R):
     _buf("ys%d" % _t, 256, F32)
 for _t in range(R - 1):
     _buf("lst%d" % _t, 16, U16)
-    _buf("rl%d" % _t, 8, U16)
+    _buf("rl%d" % _t, 10, U16)
     _buf("rq%d" % _t, 2, U16)
 
 STAGES = ["m0", "m0s", "c0", "c0s", "l0", "c1", "c1s", "l1"]
-SEMAPHORES = ["qv", "qs", "qt", "qg", "ls", "lf", "ldr", "ldm", "ldu", "ldw", "hm0", "hc0", "hc1", "hl0", "hl1", "st", "b_l0", "b_l1"]
+SEMAPHORES = ["qv", "qs", "qt", "qg", "ls", "lm", "ldr", "ldq", "lda", "ldm", "ldw", "st", "b_l0", "b_l1"]
 SEMAPHORES += ["a_" + s for s in STAGES] + ["r_" + s for s in STAGES]
 FAR, NEAR = 0, 1
 
@@ -73,17 +71,31 @@ def chips(T, topo, c):
     return out
 
 
+def places(T, topo):
+    first = T.cores[0]
+    order = [d for d in T.cores if d not in cross(T, topo, first)] + cross(T, topo, first)
+    return [order.index(d) for d in T.cores]
+
+
 def runs(T, topo, c):
-    out = []
-    for r, d in enumerate(T.cores):
-        way = NEAR if d == c or topo.may_write(d, c) else FAR
-        if out and out[-1][2] == way:
+    at = places(T, topo)
+    out, col = [], 0
+    for x in range(N):
+        d = T.cores[at.index(x)]
+        if d == c:
+            continue
+        way = NEAR if topo.may_write(d, c) else FAR
+        if out and out[-1][2] == way and out[-1][0] + out[-1][1] == x:
             out[-1][1] += 1
         else:
-            out.append([r, 1, way])
-    if any(r % 2 for r, _, _ in out):
-        out = [[0, N, FAR]]
+            out.append([x, 1, way, col + col % 2])
+        col = out[-1][3] + out[-1][1]
     return out
+
+
+def list_column(T, topo, s, c):
+    x = places(T, topo)[T.rank_of(s)]
+    return [col + x - a for a, n, _, col in runs(T, topo, c) if a <= x < a + n][0]
 
 
 def pow2(n):
@@ -93,13 +105,13 @@ def pow2(n):
     return k
 
 
-def share(topo, c, dsts):
+def share(topo, c, dsts, spare):
     off = [d for d in dsts if d not in topo.cores_of(c)]
     on = [d for d in dsts if d in topo.cores_of(c)]
     out = {}
     every = topo.engines(c, on[0]) if on else topo.engines(c, off[0])
     per = pow2(len(every) // len(dsts))
-    used = []
+    used = list(spare)
     for i, d in enumerate(off):
         out[d] = topo.engines(c, d)[per * i:per * i + per]
         used += out[d]
@@ -119,13 +131,18 @@ def kind(stage):
 
 
 def roads(T, topo, c, stage, way):
+    spare = []
     if way == NEAR:
         out = [(d, [d]) for d in direct(T, topo, c)]
     elif stage[0] == "c":
-        out = [(relay(T, topo, c, ds[(j + stage.endswith("s")) % len(ds)]), ds) for j, ds in enumerate(chips(T, topo, c))]
+        far = chips(T, topo, c)
+        i = [c in ds for ds in chips(T, topo, far[0][0])].index(True)
+        out = [(relay(T, topo, c, ds[(i + j + stage.endswith("s")) % len(ds)]), ds) for j, ds in enumerate(far)]
+        if stage.endswith("s"):
+            spare = topo.engines(c, [d for d in direct(T, topo, c) if d not in topo.cores_of(c)][0])
     else:
         out = [(relay(T, topo, c, d), [d]) for d in cross(T, topo, c)]
-    e = share(topo, c, [x for x, _ in out])
+    e = share(topo, c, [x for x, _ in out], spare)
     return [(x, e[x], ds) for x, ds in out]
 
 
@@ -135,9 +152,9 @@ def onward(T, topo, x, stage):
     if not ds:
         return []
     ds = ds[0]
-    if len(ds) == 1:
-        return [(ds[0], topo.engines(x, ds[0]), 0, len(mine), mine[0])]
     e = topo.engines(x, ds[0])
+    if len(ds) == 1:
+        return [(ds[0], e, 0, len(mine), mine[0])]
     per = pow2(len(e) // (len(mine) * len(ds)))
     out = []
     for i, s in enumerate(mine):
@@ -179,9 +196,10 @@ def relay_program(g, core, T, topo):
         t, tail, codes, base = kind(st)
         tr = []
         for d, e, a, n, s in out:
-            r = T.rank_of(s)
+            r = places(T, topo)[T.rank_of(s)]
             if st[0] == "l":
-                src, dst = T["rq%d" % t][:, a:a + n], T["rl%d" % t][:, r:r + n]
+                j = list_column(T, topo, s, d)
+                src, dst = T["rq%d" % t][:, a:a + n], T["rl%d" % t][:, j:j + n]
             else:
                 src, dst = view(T, "r" + st[:2] + tail, K * a, K * n, codes), view(T, "iw%d" % t + tail, base + K * r, K * n, codes)
             rid, pid = topo.addr(d, core)
@@ -210,7 +228,7 @@ def rank_program(g, core, T, topo):
     def waits(k, rd, wr):
         want.clear()
         for r in rd:
-            need(k, wrote.get(r, []))
+            need(k, wrote[r])
         for w in wr:
             need(k, wrote.get(w, []))
             need(k, read.get(w, []))
@@ -225,14 +243,16 @@ def rank_program(g, core, T, topo):
             wrote[w] = [tok]
             read[w] = []
 
-    def op(k, fn, rd=(), wr=()):
+    def op(k, fn, rd, wr):
+        rd, wr = rd.split(), wr.split()
         waits(k, rd, wr)
         s = "q" + k
         fn().then_inc(T.sem[s], 1)
         count[s] = count.get(s, 0) + 1
         note((s, count[s]), rd, wr)
 
-    def dmas(parts, s, rd=(), wr=()):
+    def dmas(parts, s, rd, wr):
+        rd, wr = rd.split(), wr.split()
         for k in sorted({p[0] for p in parts}):
             waits(k, rd, wr)
         for k, o, i in parts:
@@ -243,11 +263,11 @@ def rank_program(g, core, T, topo):
     v, sc, te = g.vector, g.scalar, g.tensor
     u32 = dt.uint32
 
-    def tsc(o, i, s1, s2, o1, o2, rd, wr):
-        if o2 is None:
-            op("v", lambda: v.tensor_scalar(o, i, s1, None, o1), rd, wr)
-        else:
-            op("v", lambda: v.tensor_scalar(o, i, s1, s2, o1, o2), rd, wr)
+    def ts1(o, i, s1, o1, rd, wr):
+        op("v", lambda: v.tensor_scalar(o, i, s1, None, o1), rd, wr)
+
+    def ts2(o, i, s1, o1, s2, o2, rd, wr):
+        op("v", lambda: v.tensor_scalar(o, i, s1, s2, o1, o2), rd, wr)
 
     def cp(o, i, rd, wr):
         op("v", lambda: v.tensor_copy(o, i), rd, wr)
@@ -255,106 +275,118 @@ def rank_program(g, core, T, topo):
     def ttn(o, a, b, f, rd, wr):
         op("v", lambda: v.tensor_tensor(o, a, b, f), rd, wr)
 
+    def red(o, i, f, rd, wr):
+        op("v", lambda: v.tensor_reduce(o, i, AxisListType.X, f), rd, wr)
+
     def fill(o, x, rd, wr):
         op("v", lambda: v.memset(o, x), rd, wr)
-
-    def turn(o, i, rd, wr):
-        op("v", lambda: v.transpose(o, i), rd, wr)
 
     def act(o, i, fn, rd, wr, **kw):
         op("s", lambda: sc.activation(o, i, fn, **kw), rd, wr)
 
-    def iota(o, pattern, ch, wr, base=0):
-        op("g", lambda: g.iota(o, pattern, base, ch, allow_small_or_imprecise_dtypes=True), (), [wr])
+    def iota(o, pattern, wr):
+        op("g", lambda: g.iota(o, pattern, 0, 0, allow_small_or_imprecise_dtypes=True), "", wr)
 
     def quant(name, a, b, tile, x, rd, wr):
         op("v", lambda: v.quantize_mx(T[name][:, a:b], T[name + "_s"][:, a:b], T[tile][:, x:x + 4 * (b - a)]), rd, wr)
 
+    def pickc(out, a, n, src, c, d, off, e, rd, wr):
+        op("v", lambda: v.tensor_copy(T[out][:, a:a + n].bitcast(u32), T[src][:, c:d].bitcast(u32).indirect(T[off][:, e:e + n // K])), rd, wr)
+
+    def picks(out, a, n, src, c, d, off, e, rd, wr):
+        op("s", lambda: sc.activation(T[out + "_s"][:, a:a + n], T[src + "_s"][:, c:d].indirect(T[off][:, e:e + n // K]), F.Copy), rd, wr)
+
     def pick(out, a, n, src, c, d, off, e, codes, scales, lists, wc, ws):
-        op("v", lambda: v.tensor_copy(T[out][:, a:a + n].bitcast(u32), T[src][:, c:d].bitcast(u32).indirect(T[off][:, e:e + n // K])), codes + lists, [wc])
-        op("s", lambda: sc.activation(T[out + "_s"][:, a:a + n], T[src + "_s"][:, c:d].indirect(T[off][:, e:e + n // K]), F.Copy), scales + lists, [ws])
+        pickc(out, a, n, src, c, d, off, e, codes + " " + lists, wc)
+        picks(out, a, n, src, c, d, off, e, scales + " " + lists, ws)
 
     def mm(bank, ln, la, rn, ra, start, stop, rd):
         op("t", lambda: te.matmul_mx(T[bank][:, 0:128], T[ln][:, la:la + 128], T[ln + "_s"][:, la:la + 128],
-                                     T[rn][:, ra:ra + 128], T[rn + "_s"][:, ra:ra + 128], start, stop), rd, [bank])
+                                     T[rn][:, ra:ra + 128], T[rn + "_s"][:, ra:ra + 128], start, stop), rd, bank)
 
-    parts = []
-    for a in range(4):
-        for d in range(2):
-            parts.append(("ys"[d], T.wr[32 * a + 16 * d:32 * a + 16 * d + 16, 1 - d:9 - d], T.rev[:, :]))
-    dmas(parts, "ldr", (), ["wr"])
-    dmas([("y", T.mb[:, 0:512], T.m[:, :]), ("s", T.mb[:, 512:640], T.b[:, :])], "ldm", (), ["mb"])
-    dmas([("y", T.uc[:, :], T.u[:, 0:4])], "ldu", (), ["uc"])
-    dmas([("y", T.wt[:, :], T.w[:, :])], "ldw", (), ["wt"])
+    def col(i):
+        return T.kf[:, i:i + 1]
 
-    op("g", lambda: g.iota(T.ki[:, 0:2], [[0, 2]], 0, 1), (), ["ip"])
-    iota(T.im16[:, :], [[0, 8], [1, 16]], 0, "im16")
-    iota(T.t1[:, 32:64], [[128, 2], [0, 16]], 0, "tq")
-    iota(T.ij[:, :], [[1, 128]], 0, "ij")
-    iota(T.c32[:, :], [[1, 2], [1, 16]], 0, "c32")
-    iota(T.mb[:, 640:768], [[0, 128]], 0, "xz")
-    iota(T.cf[:, 0:16], [[0, 2], [1, 8]], 0, "c8")
-    iota(T.k24[:, :], [[1, 3], [0, 8]], 0, "k24")
-    fill(T.eb[:, :], 0.0, (), ["ebz"])
-    fill(T.one[:, :], 1.0, (), ["one"])
-    tsc(T.ki[:, 2:4], T.ki[:, 0:2], 15, None, A.bitwise_and, None, ["ip"], ["i2"])
-    tsc(T.ki[:, 4:6], T.ki[:, 0:2], 4, None, A.logical_shift_right, None, ["ip"], ["i4"])
-    tsc(T.ki[:, 6:8], T.ki[:, 0:2], 22, None, A.bitwise_and, None, ["ip"], ["i6"])
-    tsc(T.ki[:, 8:10], T.ki[:, 0:2], 5, None, A.logical_shift_right, None, ["ip"], ["i8"])
-    cp(T.kf[:, 0:10], T.ki[:, :], ["ip", "i2", "i4", "i6", "i8"], ["kf"])
-    tsc(T.kf[:, 11:12], T.ki[:, 8:9], 256.0, BIG, A.mult, A.add, ["i8"], ["kc"])
-    tsc(T.t1[:, 0:32], T.t1[:, 32:64], T.kf[:, 11:12], None, A.add, None, ["tq", "kc"], ["t1"])
-    tsc(T.kf[:, 10:11], T.ki[:, 2:3], 0.5, None, A.add, None, ["i2"], ["kh"])
-    cp(T.ku[:, :], T.ki[:, :], ["ip", "i2", "i4", "i6", "i8"], ["ku"])
-    p1, k16, g16, k05 = T.kf[:, 0:1], T.kf[:, 2:3], T.kf[:, 4:5], T.kf[:, 10:11]
-    act(T.pa[:, :], T.im16[:, :], F.Abs, ["im16", "kf"], ["pa"], scale=-1.0, bias=k16)
-    for i, c in enumerate((0.5, 8.0, 0.5, 0.5)):
-        act(T.pw[:, i:512:4], T.pa[:, :], F.Relu, ["pa"], ["pw%d" % i], scale=-c, bias=c)
+    def digit(i, shift, mask):
+        ts2(T.ki[:, i:i + 1], T.ki[:, 0:1], shift, A.logical_shift_right, mask, A.bitwise_and, "ip", "i%d" % i)
 
-    def spread(dst, col, rd, both):
-        for b in range(4):
-            o, x = T[dst][:, 32 * b:32 * b + 32], T.lff[:, col + b:col + b + 1]
-            if both and b % 2:
-                tsc(o, T.one[:, 0:32], x, None, A.mult, None, ["one", rd], [dst + ".%d" % b])
-            else:
-                act(o, T.one[:, 0:32], F.Copy, ["one", rd], [dst + ".%d" % b], scale=x)
+    hc, rf, ec, n4, k8, c16, j4, k16, g16, gx, p1, hb, mx, lo, b0, b1, own, rk, ql, cn, hs = [col(i) for i in range(21)]
+    tl, mb = T.tl, T.mb
+    at = places(T, topo)
+    place = at[rank]
 
-    tsc(T.lff[:, 0:4], T.wr[:, 1:9:2], 63.75, BIG, A.subtract, A.add, ["wr"], ["h4"])
-    for b in range(4):
-        tsc(T.ah[:, 32 * b:32 * b + 32], T.t1[:, 0:32], T.lff[:, b:b + 1], None, A.is_equal, None, ["t1", "h4"], ["ah%d" % b])
-    turn(T.mk[:, :], T.ah[:, :], ["ah%d" % b for b in range(4)], ["mk"])
-    op("v", lambda: v.tensor_tensor_scan(T.cu[:, :], T.mk[:, :], T.mk[:, :], 0.0, A.add, A.max), ["mk"], ["cu"])
-    act(T.jk[:, 128:136], T.cu[:, 15:128:16], F.Sign, ["cu", "kh"], ["jb", "acc1"], scale=-1.0, bias=k05, accum_out=T.lff[:, 17:18])
-    act(T.jk[:, 0:128], T.cu[:, :], F.Sign, ["cu", "kh"], ["jk", "acc0"], scale=-1.0, bias=k05, accum_out=T.lff[:, 16:17])
-    cp(T.lff[:, 4:8], T.wr[:, 1:9:2], ["wr"], ["r4f"])
-    quant("qp", 0, 128, "pw", 0, ["pw%d" % i for i in range(4)], ["qp"])
-    tsc(T.mb[:, 641:768:4], T.c32[:, :], g16, T.lff[:, 17:18], A.is_equal, A.mult, ["c32", "kf", "acc1", "xz"], ["x1"])
-    tsc(T.lff[:, 18:19], T.lff[:, 17:18], -16.0, T.lff[:, 16:17], A.mult, A.add, ["acc0", "acc1"], ["low"])
-    tsc(T.mb[:, 640:768:4], T.c32[:, :], g16, T.lff[:, 18:19], A.is_equal, A.mult, ["c32", "kf", "low", "xz"], ["x0"])
-    quant("qx", 0, 128, "mb", 256, ["mb", "xz", "x0", "x1"], ["qx"])
-    mm("db0", "qp", 0, "qx", 0, True, True, ["qp", "qx"])
-    quant("qmb", 0, 160, "mb", 0, ["mb"], ["qmb"])
-    spread("ar", 4, "r4f", False)
-    act(T.cf[:, 48:64], T.im16[:, 0:16], F.Relu, ["im16", "kf"], ["below"], scale=-1.0, bias=k16)
-    act(T.cf[:, 96:112], T.cf[:, 0:16], F.Abs, ["c8", "kf"], ["away"], scale=-1.0, bias=g16)
-    act(T.cf[:, 80:96], T.cf[:, 48:64], F.Sign, ["below"], ["lt"])
-    act(T.hx[:, 0:16], T.cf[:, 96:112], F.Relu, ["away"], ["hm"], scale=-8.0, bias=8.0)
-    act(T.cf[:, 64:80], T.cf[:, 80:96], F.Copy, ["lt"], ["mth"], scale=-2.0 ** -24, bias=1.0)
-    act(T.lff[:, 20:24], T.uc[:, :], F.Copy, ["uc"], ["ucf"])
-    tsc(T.ls[:, 0:8], T.db0[:, 96:104], 64.0, None, A.add, None, ["db0"], ["ls"])
-    pick("mw0", 0, 128, "qmb", 0, 128, "ls", 0, ["qmb"], ["qmb"], ["ls"], "mw0.m", "mw0.m_s")
+    dmas([("y", T.wr[:, 0:1], T.rev[:, :])], "ldr", "", "wr")
+    dmas([("s", T.rr[0:1, :], T.rev[:, :])], "ldq", "", "rr")
+    dmas([("s", mb[:, 512:520], T.u[:, 0:8]), ("y", mb[:, 552:568], T.m[:, 0:16])], "lda", "", "ma")
+    dmas([("y", mb[:, 568:1064], T.m[:, 16:512]), ("s", mb[:, 1064:1192], T.b[:, :])], "ldm", "", "mb")
 
-    def send(stage, way, src, rd, local="ls"):
+    op("g", lambda: g.iota(T.ki[:, 0:2], [[0, 2]], 0, E + 1), "", "ip")
+    iota(T.er[:, :], [[1, 16], [16, 8]], "er")
+    iota(T.c32[:, :], [[128, 8], [0, 2], [2048, 2]], "c32")
+    iota(T.im16[:, :], [[0, 8], [1, 16]], "im16")
+    iota(T.k24[:, :], [[1, 3], [0, 8]], "k24")
+    iota(T.c48[:, :], [[0, 6], [128, 8]], "c48")
+    op("g", lambda: g.partition_broadcast(T.rb[:, :], T.rr[0:1, :], 128), "rr", "rb")
+    steps = [K * at[4], K * at[2], K * at[1]]
+    assert all(K * at[h] == steps[0] * (h // 4) + steps[1] * (h // 2 % 2) + steps[2] * (h % 2) for h in range(N))
+    iota(T.sg[:, 0:8], [[x, 2] for x in steps], "sg")
+    fill(T.eb[:, :], 0.0, "", "eb")
+    digit(2, 3, 127)
+    digit(3, 3, 124)
+    digit(4, 3, 15)
+    digit(5, 3, 112)
+    cp(T.kf[:, 2:4], T.ki[:, 2:4], "i2 i3", "ec n4")
+    digit(6, 3, 3)
+    ts2(mb[:, 0:512:4], T.er[:, :], ec, A.is_gt, -1.0, A.mult, "er ec", "w0")
+    ts2(mb[:, 2:512:4], T.er[:, :], ec, A.is_equal, 32.0, A.mult, "er ec", "w2")
+    ts2(mb[:, 1:512:4], T.er[:, :], -3.0, A.add, n4, A.is_gt, "er n4", "w1")
+    ts1(mb[:, 3:512:4], T.er[:, :], n4, A.is_ge, "er n4", "w3")
+    act(tl[:, 512:608], T.eb[:, 0:96], F.Copy, "eb", "xz", scale=0.0)
+    act(tl[:, 0:512], T.eb[:, 0:512], F.Copy, "eb", "cw", scale=0.0, bias=1.0)
+
+    ts2(hc, T.wr[:, 0:1], 63.75, A.subtract, BIG, A.add, "wr", "hc")
+    cp(T.kf[:, 4:7], T.ki[:, 4:7], "i4 i5 i6", "k8 c16 j4")
+    ts2(mb[:, 520:552], T.c32[:, :], BIG, A.add, hc, A.is_equal, "c32 hc", "x1")
+    quant("q1", 0, 128, "mb", 0, "w0 w1 w2 w3", "q1")
+    quant("qa", 0, 128, "mb", 56, "w0 w1 w2 w3 ma x1", "qa")
+    mm("db0", "q1", 0, "qa", 0, True, True, "q1 qa")
+    act(tl[:, 512:544:4], mb[:, 520:552:4], F.Copy, "x1 k8 xz", "x2", scale=k8)
+    act(tl[:, 544:576:4], mb[:, 520:552:4], F.Copy, "x1 c16 xz", "x3", scale=c16)
+    cp(rf, T.wr[:, 0:1], "wr", "rf")
+    ts2(hb, hc, BIG, A.subtract, -1.0 / 1024, A.mult, "hc", "hb")
+    digit(7, 0, 15)
+    digit(8, 4, 7)
+    red(mx, T.db0[:, 116:124], A.max, "db0", "mx")
+    ts2(T.mk[:, 3:96:4], T.k24[:, :], 1.0, A.add, j4, A.is_equal, "k24 j4", "mk3")
+    ts2(tl[:, 0:512:4], T.im16[:, :], mx, A.add, 32.0, A.is_equal, "im16 mx", "cw")
+    ts2(T.mk[:, 1:96:4], T.k24[:, :], j4, A.is_equal, -1.0, A.mult, "k24 j4", "mk1")
+    quant("qc", 0, 152, "tl", 0, "cw xz x2 x3", "qc")
+    mm("db1", "qc", 0, "qc", 16, True, False, "qc")
+    mm("db1", "qc", 0, "qc", 24, False, True, "qc")
+    quant("qmb", 0, 160, "mb", 552, "ma mb", "qmb")
+    digit(9, 0, 112)
+    digit(10, 0, 127)
+    act(tl[:, 800:1152], T.eb[:, 0:352], F.Copy, "eb", "gz", scale=0.0)
+    act(T.nb[:, 516:552], T.eb[:, 0:36], F.Copy, "eb", "xc0", scale=0.0)
+    act(T.eb[:, 3:512:4], mb[:, 2:512:4], F.Copy, "w2", "eb", scale=1.0 / 32)
+    act(T.mk[:, 2:96:4], T.mk[:, 3:96:4], F.Copy, "mk3", "mk2", scale=-1.0 / 32)
+    cp(T.ls[:, 0:8], T.db1[:, 112:120], "db1", "ls")
+    cp(T.li[:, 0:8], T.db1[:, 112:120], "db1", "li")
+    pick("mw0", 0, 128, "qmb", 0, 128, "ls", 0, "qmb", "qmb", "ls", "mw0.m", "mw0.m_s")
+
+    def send(stage, way, src, rd):
         t, tail, codes, base = kind(stage)
         i = peers(T, topo, core).index(core)
+        local = "lm" if stage[0] == "m" else "ls"
         waits("g", rd, ())
         tr = []
         for x, e, ds in roads(T, topo, core, stage, way):
             n = len(ds)
             if stage[0] == "l":
-                dst = T["rl%d" % t][:, rank:rank + 1] if way == NEAR else T["rq%d" % t][:, i:i + 1]
+                j = list_column(T, topo, core, ds[0])
+                dst = T["rl%d" % t][:, j:j + 1] if way == NEAR else T["rq%d" % t][:, i:i + 1]
             elif way == NEAR:
-                dst = view(T, "iw%d" % t + tail, base + K * rank, K, codes)
+                dst = view(T, "iw%d" % t + tail, base + K * place, K, codes)
             else:
                 dst = view(T, "r" + stage[:2] + tail, K * n * i, K * n, codes)
             rid, pid = topo.addr(x, core)
@@ -364,220 +396,216 @@ def rank_program(g, core, T, topo):
         g.remote_dma_fused(tr, local_sem=T.sem[local])
         count.update(landed(T, topo, core, stage))
 
-    def columns(stage, way, local="ls"):
-        t, tail, codes, base = kind(stage)
-        m = "mw%d" % t
-        send(stage, way, lambda h, n: view(T, m + tail, base + K * h, K * n, codes), [m + (".c" if base else ".m") + tail], local)
+    def exchange(x):
+        t, _, _, base = kind(x)
+        m, part = "mw%d" % t, ".c" if base else ".m"
+        for way in (FAR, NEAR):
+            for st, tail in ((x, ""), (x + "s", "_s")):
+                send(st, way, lambda h, n: view(T, m + tail, base + K * h, K * n, not tail), [m + part + tail])
+        for st, tail in ((x, ""), (x + "s", "_s")):
+            wrote["iw%d%s%s" % (t, part, tail)] = [("a_" + st, count["a_" + st])]
 
-    def home(stage, after):
-        t, _, _, base = kind(stage)
-        m, iw, part, at = "mw%d" % t, "iw%d" % t, ".c" if base else ".m", base + K * rank
-        dmas([("y", view(T, iw, at, K, True), view(T, m, at, K, True)),
-              ("y", view(T, iw + "_s", at, K, False), view(T, m + "_s", at, K, False))], "h" + stage, [m + part, m + part + "_s"] + after, ["home"])
-        h = wrote.pop("home")
-        for x, y in (("", ""), ("s", "_s")):
-            wrote[iw + part + y] = [("a_" + stage + x, count["a_" + stage + x])] + h
-
-    for way, local in ((FAR, "lf"), (NEAR, "ls")):
-        for st in ("m0", "m0s"):
-            columns(st, way, local)
-    wrote["left"] = [("lf", count["lf"])]
-    home("m0", ["left"])
-    iota(T.pb[:, :], [[0, 512]], 0, "pb", 1)
-    iota(T.nb[:, :], [[0, 516]], 0, "nbz")
-    iota(T.gb[:, :], [[0, 512]], 0, "gb")
-    iota(T.cf[:, 16:32], [[16, 8], [0, 2]], 0, "h16")
-
-    turn(T.rb[:, :], T.ar[:, :], ["ar.%d" % b for b in range(4)], ["rb"])
-    for b in range(4):
-        act(T.js[:, 128 * b:128 * b + 128], T.rb[:, :], F.Sign, ["rb", "r4f"], ["js%d" % b, "sa%d" % b], scale=-1.0, bias=T.lff[:, 4 + b:5 + b], accum_out=T.lff[:, 8 + b:9 + b])
-    tsc(T.li[:, :], T.db0[:, 96:128], 64.0, None, A.add, None, ["db0"], ["li"])
-    cp(T.ld[:, :], T.li[:, :].indirect(T.ku[:, 6:8]), ["li", "ku"], ["ld"])
-    tsc(T.l4[:, 24:32], T.li[:, 0:8], 2, None, A.logical_shift_right, None, ["li"], ["l2"])
-    tsc(T.l4[:, 0:24], T.ld[:, 0:24], 124, None, A.bitwise_and, None, ["ld"], ["l4"])
-    cp(T.ls[:, 8:16], T.l4[:, 24:32], ["l2"], ["lb"])
-    ttn(T.fw[:, 0:24], T.l4[:, 0:24], T.k24[:, :], A.add, ["l4", "k24"], ["fw"])
-    ttn(T.fw[:, 24:48], T.fw[:, 0:24], T.ld[:, 0:24], A.is_ge, ["fw", "ld"], ["fc"])
-    ttn(T.fw[:, 48:72], T.fw[:, 0:24], T.fw[:, 24:48], A.add, ["fw", "fc"], ["fk"])
-    cp(T.fd[:, :], T.fw[:, 48:72], ["fk"], ["fd"])
-    pick("bb", 0, 128, "qmb", 128, 160, "ls", 8, ["qmb"], ["qmb"], ["lb"], "bb", "bb_s")
-    tsc(T.lff[:, 12:16], T.lff[:, 8:12], 0.5, 63.5, A.mult, A.add, ["sa%d" % b for b in range(4)], ["s4"])
-    spread("asl", 12, "s4", True)
-    tsc(T.eb[:, 3:512:4], T.ij[:, :], p1, None, A.is_equal, None, ["ij", "kf", "ebz"], ["ebh"])
-    turn(T.slb[:, :], T.asl[:, :], ["asl.%d" % b for b in range(4)], ["slb"])
-    cp(T.dk[:, 0:192], T.slb[:, :].indirect(T.fd[:, 0:12]), ["slb", "fd"], ["dk0"])
-    act(T.dk[:, 192:384], T.slb[:, :].indirect(T.fd[:, 12:24]), F.Copy, ["slb", "fd"], ["dk1"])
+    exchange("m0")
+    iota(T.ij[:, :], [[1, 128]], "ij")
+    wrote["left"] = [("lm", count["lm"])]
+    dmas([("y", T.wt[:, :], T.w[:, :])], "ldw", "left", "wt")
 
     def unpacking(b):
-        quant("ep", 128 * b, 128 * b + 128, "eb", 3 - b, ["ebz", "ebh"], ["ep%d" % b])
+        quant("ep", 128 * b, 128 * b + 128, "eb", 3 - b, "eb", "ep%d" % b)
 
-    for b in (0, 1):
-        unpacking(b)
-    turn(T.dkt[:, :], T.dk[:, :], ["dk0", "dk1"], ["dkt"])
-    cp(T.lf[:, :], T.dkt[:, 0:384:16], ["dkt"], ["lf"])
-    for b in (2, 3):
-        unpacking(b)
-    act(T.pb[:, 0:512:4], T.pa[:, :], F.Relu, ["pa", "pb"], ["pb0"], scale=-128.0, bias=128.0)
-    act(T.pb[:, 2:512:4], T.im16[:, :], F.Copy, ["im16", "pb"], ["pb2"])
+    def negative(b):
+        quant("en", 128 * b, 128 * b + (138 if b == 3 else 128), "nb", 3 - b, "nb xc0 xc1 xc2" if b == 3 else "nb", "en%d" % b)
 
-    def tile_u(t):
-        act(T.ub[:, t:512:4], T.one[:, :], F.Copy, ["one", "ucf"], ["ub%d" % t], scale=T.lff[:, 20 + t:21 + t])
-
-    for b in (0, 1):
-        tile_u(b)
+    ts1(T.jk[:, 0:128], T.rb[:, :], rf, A.is_lt, "rb rf", "jk")
+    act(T.jk[:, 128:256], T.jk[:, 0:128], F.Identity, "jk hb", "jl lo", bias=hb, accum_out=lo)
+    ttn(T.sg[:, 8:16], mb[:, 520:552:4], T.sg[:, 0:8], A.mult, "x1 sg", "sh")
+    ttn(T.mk[:, 0:96:4], T.mk[:, 1:96:4], T.mk[:, 3:96:4], A.add, "mk1 mk3", "mk0")
+    ts1(T.li[:, 8:16], T.li[:, 0:8], 2, A.logical_shift_right, "li", "l2")
+    red(hs, T.sg[:, 8:16], A.add, "sh", "hs")
+    cp(T.ow[:, 0:1], T.li[:, rank:rank + 1], "li", "ow0")
+    cp(T.ls[:, 8:16], T.li[:, 8:16], "l2", "lb")
+    ts1(tl[:, 704:800], T.mk[:, :], hs, A.mult, "mk0 mk1 mk2 mk3 hs", "xh")
+    ts1(tl[:, 608:704], T.mk[:, :], lo, A.mult, "mk0 mk1 mk2 mk3 lo", "xl")
+    act(T.lif[:, :], T.db1[:, 112:128], F.Copy, "db1 ls li", "lif")
+    unpacking(0)
+    quant("qb", 0, 128, "tl", 288, "cw xz x2 x3 xl xh", "qb")
+    mm("db2", "q1", 0, "qb", 0, True, True, "q1 qb")
+    ts2(T.oh[:, :], T.c48[:, :], BIG, A.add, hc, A.is_equal, "c48 hc", "oh")
+    pick("bb", 0, 128, "qmb", 128, 160, "ls", 8, "qmb", "qmb", "lb", "bb", "bb_s")
+    act(T.nb[:, 0:516], T.eb[:, 0:516], F.Copy, "eb", "nb", scale=-1.0)
+    act(T.nb[:, 521:552:4], T.im16[:, 0:8], F.Copy, "im16 xc0", "xc1", scale=0.0, bias=-16.0)
+    ttn(tl[:, 800:992:4], T.db2[:, 80:128], T.oh[:, :], A.mult, "db2 oh gz", "x4")
+    unpacking(1)
+    quant("q3", 0, 152, "tl", 384, "cw xz x2 x3 xl xh gz x4", "q3")
+    mm("db3", "qc", 0, "q3", 0, True, False, "qc q3")
+    mm("db3", "qc", 0, "q3", 24, False, True, "qc q3")
+    unpacking(2)
+    unpacking(3)
+    cp(T.lf[:, :], T.db3[:, 104:128], "db3", "lf")
 
     def prefill_m(t):
         for b in range(4):
-            mm("db%d" % b, "en", 128 * b, "mw%d" % t, 0, True, False, ["en%d" % b, "mw%d.m" % t, "mw%d.m_s" % t])
+            mm("db%d" % b, "en", 128 * b, "mw%d" % t, 0, True, False, "en%d mw%d.m mw%d.m_s" % (b, t, t))
 
     def prefill_b():
         for b in range(4):
-            mm("zb%d" % b, "ep", 128 * b, "bb", 0, True, False, ["ep%d" % b, "bb", "bb_s"])
+            mm("zb%d" % b, "ep", 128 * b, "bb", 0, True, False, "ep%d bb bb_s" % b)
 
     prefill_b()
+    cp(T.kf[:, 7:11], T.ki[:, 7:11], "i7 i8 i9 i10", "k16 g16 gx p1")
+    fill(T.zu[:, :], 18, "", "zu")
+    pick("iw0", K * place, K, "qmb", 0, 128, "ow", 0, "qmb", "qmb", "ow0", "iw0.o", "iw0.o_s")
+    ts2(T.ct[:, :], T.im16[:, :], k16, A.is_le, -2.0 ** -24, A.mult, "im16 k16", "ct")
+    ts2(T.nb[:, 520:552:4], T.im16[:, 0:8], g16, A.is_equal, 256.0, A.mult, "im16 g16 xc0", "xc2")
+    picks("qu", 0, 128, "qa", 96, 128, "zu", 0, "qa zu", "qu_s")
+    act(T.cm[:, :], T.ct[:, :], F.Copy, "ct", "cm", bias=1.0)
+    for b in (0, 1):
+        negative(b)
     seg = runs(T, topo, core)
-    flags = ["gb", "gb0", "gb1", "gb3", "gb4", "gb5", "gb6", "gb7"]
 
     def inw(t, tail):
-        return ["iw%d.m%s" % (t, tail)] if t == 0 else ["iw%d.m%s.%d" % (t, tail, r) for r, _, _ in seg]
+        return "iw%d.o%s " % (t, tail) + ("iw0.m" + tail if t == 0 else " ".join("iw%d.m%s.%d" % (t, tail, r[0]) for r in seg))
 
     def results(i, src, m):
-        act(T["ys%d" % i][:, 0:128], T[src + "0"][:, 0:128].indirect(T.ln[:, 0:8]), F.Copy, [src + "0" + m, "ln"], ["ys%d.0" % i])
-        cp(T["ys%d" % i][:, 128:256], T[src + "1"][:, 0:128].indirect(T.ln[:, 0:8]), [src + "1" + m, "ln"], ["ys%d.1" % i])
-        dmas([("y", T.y[:, 256 * i:256 * i + 256], T["ys%d" % i][:, :])], "st", ["ys%d.0" % i, "ys%d.1" % i], ())
+        act(T["ys%d" % i][:, 0:128], T[src + "0"][:, 0:128].indirect(T.ln[:, 0:8]), F.Copy, src + "0" + m + " ln", "ys%d.0" % i)
+        cp(T["ys%d" % i][:, 128:256], T[src + "1"][:, 0:128].indirect(T.ln[:, 0:8]), src + "1" + m + " ln", "ys%d.1" % i)
+        dmas([("y", T.y[:, 256 * i:256 * i + 256], T["ys%d" % i][:, :])], "st", "ys%d.0 ys%d.1" % (i, i), "")
+
+    def natural(bank, stop):
+        mm(bank, "qk", 0, "q0", 0, True, False, "qk q0")
+        mm(bank, "qk", 0, "q0", 8, False, stop, "qk q0")
+
+    def products(m, a, rd):
+        for o in range(O):
+            mm("zb%d" % (2 + o), "qw", 128 * o, m, a, True, True, "qw " + rd)
 
     for t in range(R):
         iw, mw, f = "iw%d" % t, "mw%d" % t, "f%d" % t
-        nw, last = "mw%d" % (t + 1), t == R - 1
+        nw, ni, last = "mw%d" % (t + 1), "iw%d" % (t + 1), t == R - 1
+        both, both_s = mw + ".m " + mw + ".c", mw + ".m_s " + mw + ".c_s"
         for k in range(3):
-            pick(f, 128 * k, 128, iw, 0, 128, "lf", 8 * k, inw(t, ""), inw(t, "_s"), ["lf"], f + ".%d" % k, f + "s.%d" % k)
+            pick(f, 128 * k, 128, iw, 0, 128, "lf", 8 * k, inw(t, ""), inw(t, "_s"), "lf", f + ".%d" % k, f + "s.%d" % k)
         for k in range(3):
             for b in range(4):
-                mm("zb%d" % b, "ep", 128 * b, f, 128 * k, False, k == 2, ["ep%d" % b, f + ".%d" % k, f + "s.%d" % k])
+                mm("zb%d" % b, "ep", 128 * b, f, 128 * k, False, k == 2, "ep%d %s.%d %ss.%d" % (b, f, k, f, k))
         if t == 0:
-            tsc(T.nb[:, 3:512:4], T.ij[:, :], p1, -1.0, A.is_equal, A.mult, ["ij", "kf", "nbz"], ["nbh"])
-            for b in range(4):
-                quant("en", 128 * b, 128 * b + 128, "nb", 3 - b, ["nbz", "nbh"], ["en%d" % b])
-            prefill_m(0)
             for b in (2, 3):
-                tile_u(b)
-            act(T.ub[:, 4:8], T.uc[:, :], F.Copy, ["uc"] + ["ub%d" % b for b in range(4)], ["ubn"], scale=-1.0)
+                negative(b)
+            prefill_m(0)
         if t == 1:
-            quant("qk", 0, 128, "pk", 0, ["pk%d" % i for i in range(4)], ["qk"])
-            quant("qw", 0, 256, "wt", 0, ["wt"], ["qw"])
+            quant("qw", 0, 256, "wt", 0, "wt", "qw")
         if last:
-            quant("qn", 0, 128, "pn", 0, ["pnz", "pn0", "pn3"], ["qn"])
             results(1, "yw", ".m")
         for b in range(4):
             if b % 2:
-                tsc(T.z[:, b:512:4], T["zb%d" % b][:, 0:128], 0.25, None, A.mult, None, ["zb%d" % b], ["z%d" % b])
+                ts1(T.z[:, b:512:4], T["zb%d" % b][:, 0:128], 0.25, A.mult, "zb%d" % b, "z%d" % b)
             else:
-                act(T.z[:, b:512:4], T["zb%d" % b][:, 0:128], F.Copy, ["zb%d" % b], ["z%d" % b], scale=0.25)
-        quant(mw, 128, 256, "z", 0, ["z%d" % b for b in range(4)], [mw + ".c", mw + ".c_s"])
+                act(T.z[:, b:512:4], T["zb%d" % b][:, 0:128], F.Copy, "zb%d" % b, "z%d" % b, scale=0.25)
+        quant(mw, 128, 256, "z", 0, "z0 z1 z2 z3", mw + ".c " + mw + ".c_s")
         for b in range(4):
-            mm("db%d" % b, "ep", 128 * b, mw, 128, False, True, ["ep%d" % b, mw + ".c"])
+            mm("db%d" % b, "ep", 128 * b, mw, 128, False, True, "ep%d %s.c" % (b, mw))
         if t == 0:
-            quant("qu", 0, 128, "ub", 0, ["ubn"] + ["ub%d" % b for b in range(4)], ["qu"])
-            quant("pc", 0, 128, "pb", 0, ["pb", "pb0", "pb2"], ["pc"])
-            act(T.gb[0:1, 1:32:4], T.one[0:1, 0:8], F.Copy, ["one", "gb"], ["gb1"], scale=float(K * rank))
-            act(T.gb[0:1, 33:64:4], T.cf[0:1, 16:32:2], F.Copy, ["h16", "gb"], ["gb3"])
-            act(T.gb[0:1, 2:64:4], T.one[0:1, 0:16], F.Copy, ["one", "gb"], ["gb4"])
-        if not last:
-            for way in (FAR, NEAR):
-                for x in ("c%d", "c%ds"):
-                    columns(x % t, way)
+            pickc("qu", 0, 128, "qa", 96, 128, "zu", 0, "qa zu", "qu")
+        if t == 1:
+            products(mw, 0, mw + ".m " + mw + ".m_s")
+        if last:
+            products(mw, 128, mw + ".c")
+        else:
+            exchange("c%d" % t)
         for b in range(4):
             if b % 2:
-                cp(T.dd[:, b:512:4], T["db%d" % b][:, 0:128], ["db%d" % b], ["dd%d" % b])
+                cp(T.dd[:, b:512:4], T["db%d" % b][:, 0:128], "db%d" % b, "dd%d" % b)
             else:
-                act(T.dd[:, b:512:4], T["db%d" % b][:, 0:128], F.Copy, ["db%d" % b], ["dd%d" % b])
-        quant("qd", 0, 128, "dd", 0, ["dd%d" % b for b in range(4)], ["qd"])
+                act(T.dd[:, b:512:4], T["db%d" % b][:, 0:128], F.Copy, "db%d" % b, "dd%d" % b)
+        quant("qd", 0, 128, "dd", 0, "dd0 dd1 dd2 dd3", "qd")
+        if t == 1:
+            natural("db0", True)
+            cp(T.yv1[:, :], T.zb3[:, 0:128], "zb3", "yv1")
+            act(T.yv0[:, :], T.zb2[:, 0:128], F.Copy, "zb2", "yv0")
+            cp(T.ln[:, 0:8], T.db0[:, 120:128], "db0", "ln")
         if last:
-            for o in range(O):
-                mm("zb%d" % (2 + o), "qw", 128 * o, mw, 128, True, True, ["qw", mw + ".c"])
-            cp(T.yw0[:, 128:256], T.zb2[:, 0:128], ["zb2"], ["yw0.c"])
-        mm("zb1", "qu", 0, "qd", 0, True, True, ["qu", "qd"])
-        mm("zb0", "qd", 0, "qu", 0, True, True, ["qu", "qd"])
-        act(T.sx[:, :], T.zb1[:, 0:128], F.Abs, ["zb1"], ["sx"], bias=EPS)
-        tsc(T.sm[:, 0:1], T.zb0[:, 0:1], T.zb0[:, 1:2], EPS, A.max, A.add, ["zb0"], ["sc"])
-        tsc(T.tt[:, 16:32], T.cf[:, 64:80], T.sm[:, 0:1], None, A.mult, None, ["mth", "sc"], ["th"])
-        ttn(T.tt[:, 32:48], T.sx[:, :].indirect(T.ku[:, 0:1]), T.tt[:, 16:32], A.is_gt, ["sx", "ku", "th"], ["kk"])
-        op("v", lambda: v.tensor_reduce(T.sm[:, 2:3], T.tt[:, 32:48], AxisListType.X, A.add), ["kk"], ["rk"])
+            natural("db0", False)
+            cp(T.yw0[:, 128:256], T.zb2[:, 0:128], "zb2", "yw0.c")
+            act(T.yw1[:, 128:256], T.zb3[:, 0:128], F.Copy, "zb3", "yw1.c")
+        mm("zb0", "qd", 0, "qu", 0, True, True, "qu qu_s qd")
+        mm("zb1", "qu", 0, "qd", 0, True, True, "qu qu_s qd")
         if t == 0:
-            tsc(T.gb[:, 0:64:4], T.hx[:, 0:16], T.sm[:, 2:3], None, A.is_gt, None, ["hm", "rk", "gb"], ["gb0"])
-        else:
-            tsc(T.gb[:, 0:132:4], T.hx[:, 0:33], T.sm[:, 2:3], None, A.is_gt, None, ["hm", "hn", "h0", "h8", "rk", "gb"], ["gb0"])
-        quant("qg", 0, 128, "gb", 0, flags, ["qg"])
+            ts2(T.ku[:, 0:8], T.im16[:, 0:8], 0.0, A.mult, p1, A.add, "im16 p1", "ku")
+            ts1(b0, k16, float(K * place), A.add, "k16", "b0")
+            ts1(b1, k16, float(K * place + E), A.add, "k16", "b1")
+        act(own, T.zb0[:, 0:1], F.Abs, "zb0", "own", bias=EPS)
+        act(T.sx[:, :], T.zb1[:, 0:128], F.Abs, "zb1", "sx", bias=EPS)
         if last:
-            act(T.yw1[:, 128:256], T.zb3[:, 0:128], F.Copy, ["zb3"], ["yw1.c"])
-            mm("db0", "qk", 0, "qg", 0, True, True, ["qk", "qg"])
-            mm("db1", "qg", 0, "qn", 0, True, True, ["qg", "qn"])
-            cp(T.ln[:, 8:16], T.db0[:, 16:24], ["db0"], ["nl"])
-            pick("nt", 0, 128, mw, 0, 256, "ln", 8, [mw + ".m", mw + ".c"], [mw + ".m_s", mw + ".c_s"], ["nl"], "nt", "nt_s")
-            act(T.ys2[:, 0:128], T.yw0[:, :].indirect(T.ln[:, 8:16]), F.Copy, ["yw0.m", "yw0.c", "nl"], ["ys2.0"])
-            cp(T.ys2[:, 128:256], T.yw1[:, :].indirect(T.ln[:, 8:16]), ["yw1.m", "yw1.c", "nl"], ["ys2.1"])
-            cp(T.ups[:, :], T.db1[:, 0:128], ["db1"], ["ups"])
-            dmas([("y", T.oc[:, :], view(T, "nt", 0, 128, True))], "st", ["nt"], ())
-            dmas([("y", T.osc[4 * k:4 * k + 4, :], T["nt_s"][32 * k:32 * k + 4, :]) for k in range(4)], "st", ["nt_s"], ())
-            dmas([("s", T.y[:, 512:640], T.ys2[:, 0:128])], "st", ["ys2.0"], ())
-            dmas([("y", T.y[:, 640:768], T.ys2[:, 128:256])], "st", ["ys2.1"], ())
-            dmas([("s", T.up[:, :], T.ups[32:33, :])], "st", ["ups"], ())
+            ts1(T.th[:, 0:16], T.cm[:, 0:16], own, A.mult, "cm own", "th")
+            ttn(T.kk[:, :], T.sx[:, :].indirect(T.ku[:, 0:1]), T.th[:, 0:16], A.is_gt, "sx ku th", "kk")
+            red(rk, T.kk[:, :], A.add, "kk", "rk")
+            ts2(tl[:, 1056:1088:4], T.hx[:, 8:16], rk, A.is_gt, 128.0, A.mult, "hx rk gz", "gf")
+            act(tl[:, 993:994], rk, F.Sign, "rk gz", "gs", scale=-1.0, bias=8.5)
+            quant("qg", 0, 128, "tl", 576, "xz xl xh gz x4 gf gs gc", "qg")
+            mm("db0", "qk", 0, "qg", 0, False, True, "qk qg")
+            cp(T.ln[:, 8:16], T.db0[:, 120:128], "db0", "nl")
+            cp(T.ups[:, 0:1], T.db0[:, 104:105], "db0", "ups")
+            pick("nt", 0, 128, mw, 0, 256, "ln", 8, both, both_s, "nl", "nt", "nt_s")
+            act(T.ys2[:, 0:128], T.yw0[:, :].indirect(T.ln[:, 8:16]), F.Copy, "yw0.m yw0.c nl", "ys2.0")
+            cp(T.ys2[:, 128:256], T.yw1[:, :].indirect(T.ln[:, 8:16]), "yw1.m yw1.c nl", "ys2.1")
+            planes = [("yyss"[k], T.osc[4 * k:4 * k + 4, :], T["nt_s"][32 * k:32 * k + 4, :]) for k in range(4)]
+            dmas([("y", T.up[:, :], T.ups[:, 0:1])], "st", "ups", "")
+            dmas([("y", T.oc[:, :], view(T, "nt", 0, 128, True))], "st", "nt", "")
+            dmas(planes[:2], "st", "nt_s", "")
+            dmas([("s", T.y[:, 512:640], T.ys2[:, 0:128])], "st", "ys2.0", "")
+            dmas([("y", T.y[:, 640:768], T.ys2[:, 128:256])], "st", "ys2.1", "")
+            dmas(planes[2:], "st", "nt_s", "")
             break
         lst = "lst%d" % t
-        mm("zb2", "pc", 0, "qg", 0, True, True, ["pc", "qg"])
+        ts1(T.th[:, :], T.cm[:, :], own, A.mult, "cm own", "th")
+        ttn(tl[:, 0:512:4], T.sx[:, :].indirect(T.ku[:, 0:8]), T.th[:, :], A.is_gt, "sx ku th", "cw")
+        quant("qr", 0, 128, "tl", 0, "cw", "qr")
+        mm("zb2", "qr", 0, "en", 394, True, True, "qr en3")
         if t == 0:
-            tsc(T.sm[:, 6:7], T.sm[:, 2:3], 8.0, None, A.is_lt, None, ["rk"], ["cnt"])
-        cp(T[lst][:, :], T.zb2[:, 0:16], ["zb2"], [lst])
+            ts2(T.fl[:, 48:56], T.im16[:, 0:8], 16.0, A.mult, k16, A.add, "im16 k16", "pb")
+            cp(T.ku[:, 8:9], T.ki[:, 8:9], "i8", "kg")
+        ts2(T[lst][:, 0:8], T.zb2[:, 120:128], b0, A.max, b1, A.min, "zb2 b0 b1", lst)
         for way in (FAR, NEAR):
             send("l%d" % t, way, lambda h, n: T[lst][:, h:h + n], [lst])
-        dmas([("y", T["rl%d" % t][:, rank:rank + 1], T[lst][:, rank:rank + 1])], "hl%d" % t, [lst], ["home"])
-        h = wrote.pop("home")
         for way in (FAR, NEAR):
             s = arrival("l%d" % t, way)
-            wrote["rl%d.%d" % (t, way)] = [(s, count[s])] + (h if way == NEAR else [])
-        if len(seg) == 1:
-            wrote["rl%d.%d" % (t, FAR)] += wrote["rl%d.%d" % (t, NEAR)]
-        home("c%d" % t, [lst])
-        pick(nw, 0, 128, mw, 0, 256, lst, 8, [mw + ".m", mw + ".c"], [mw + ".m_s", mw + ".c_s"], [lst], nw + ".m", nw + ".m_s")
-        prefill_m(t + 1)
+            wrote["rl%d.%d" % (t, way)] = [(s, count[s])]
+        ts2(T.fl[:, 0:8], T.zb2[:, 120:128], 128.0, A.is_gt, 128.0, A.mult, "zb2", "fa")
         if t == 0:
-            iota(T.pn[:, :], [[0, 512]], 0, "pnz")
-            iota(T.hx[:, 24:32], [[0, 8]], 0, "h0")
-            iota(T.hx[:, 32:34], [[0, 2]], 0, "h8", 8)
-            cp(T.eq[:, :], T.li[:, :].indirect(T.ku[:, 4:5]), ["li", "ku"], ["eq"])
-            tsc(T.ei[:, 0:1], T.eq[:, 0:1], 15, None, A.bitwise_and, None, ["eq"], ["e0"])
-            tsc(T.ei[:, 1:2], T.eq[:, 0:1], 4, None, A.logical_shift_right, None, ["eq"], ["e1"])
-            cp(T.ef[:, 0:2], T.ei[:, :], ["e0", "e1"], ["ef"])
-            tsc(T.hk[:, 0:128], T.im16[:, :], T.ef[:, 0:1], None, A.is_equal, None, ["im16", "ef"], ["hk"])
-            for i, c in enumerate((128.0, 16.0, 1.0, 1.0)):
-                act(T.pk[:, i:512:4], T.hk[:, 0:128], F.Copy, ["hk"], ["pk%d" % i], scale=c)
-            cp(T.ef[:, 2:3], T.eq[:, 0:1], ["eq"], ["ee"])
-            tsc(T.hk[:, 128:256], T.ij[:, :], T.ef[:, 2:3], None, A.is_equal, None, ["ij", "ee"], ["hnn"])
-            for i in (0, 3):
-                act(T.pn[:, i:512:4], T.hk[:, 128:256], F.Copy, ["hnn", "pnz"], ["pn%d" % i])
-            tsc(T.oh[:, :], T.cf[:, 0:16], T.ef[:, 1:2], None, A.is_equal, None, ["c8", "ef"], ["oh"])
-            tsc(T.hx[:, 16:24], T.oh[:, 0:8], 8.0, None, A.mult, None, ["oh"], ["hn"])
-            tsc(T.gb[:, 65:128:4], T.oh[:, :], g16, None, A.mult, None, ["oh", "kf", "gb", "qg"], ["gb6"])
-            tsc(T.gb[:, 66:128:4], T.oh[:, :], k16, None, A.mult, None, ["oh", "kf", "gb", "qg"], ["gb7"])
+            cp(T.eq[:, 0:16], T.lif[:, 0:8].indirect(T.ku[:, 8:9]), "lif kg", "e0")
+            act(T.eq[:, 16:32], T.lif[:, 8:16].indirect(T.ku[:, 8:9]), F.Copy, "lif kg", "e1")
+        ttn(T.fl[:, 8:16], T.fl[:, 0:8], T.fl[:, 48:56], A.add, "fa pb", "fb")
+        ttn(T.fl[:, 16 + 8 * t:24 + 8 * t], T.fl[:, 0:8], T.nb[:, 520:552:4], A.mult, "fa xc2", "fm%d" % t)
+        cp(T[lst][:, 8:16], T.fl[:, 8:16], "fb", lst + "o")
+        cp(T.ow[:, 2 * t + 2:2 * t + 3], T.fl[:, 8 + rank:9 + rank], "fb", "ow%d" % (t + 1))
+        if t == 0:
+            ttn(ql, T.eq[:, 0:1], T.eq[:, 16:17], A.subtract, "e0 e1", "ql")
+        pick(nw, 0, 128, mw, 0, 256, lst, 8, both, both_s, lst + "o", nw + ".m", nw + ".m_s")
+        prefill_m(t + 1)
+        pick(ni, K * place, K, mw, 0, 256, "ow", 2 * t + 2, both, both_s, "ow%d" % (t + 1), ni + ".o", ni + ".o_s")
+        if t == 0:
+            ts1(T.tk[:, 0:512:4], T.im16[:, :], ql, A.is_equal, "im16 ql", "tk0")
+            ts2(T.tk[:, 1:512:4], T.ij[:, :], T.eq[:, 0:1], A.is_equal, 0.5, A.mult, "ij e0", "tk1")
+            ts2(T.hx[:, 0:8], T.im16[:, 0:8], 16.0, A.mult, T.eq[:, 16:17], A.is_equal, "im16 e1", "ho")
+            for i in (2, 3):
+                act(T.tk[:, i:512:4], T.tk[:, 1:512:4], F.Copy, "tk1", "tk%d" % i)
+            act(tl[:, 1088:1120:4], T.hx[:, 0:8], F.Copy, "ho k16 gz", "g1", scale=k16)
+            act(tl[:, 1120:1152:4], T.hx[:, 0:8], F.Copy, "ho gx gz", "g2", scale=gx)
+            act(T.hx[:, 8:16], T.hx[:, 0:8], F.Copy, "ho", "hx", scale=9.0)
+            quant("qk", 0, 128, "tk", 0, "tk0 tk1 tk2 tk3", "qk")
+            quant("q0", 0, 136, "tl", 608, "xl xh gz x4 g1 g2", "q0")
         else:
-            mm("zb3", "qk", 0, "qg", 0, True, True, ["qk", "qg"])
-            for o in range(O):
-                mm("zb%d" % o, "qw", 128 * o, mw, 0, True, True, ["qw", mw + ".m", mw + ".m_s"])
-            cp(T.ln[:, 0:8], T.zb3[:, 24:32], ["zb3"], ["ln"])
-            for o in range(O):
-                mm("zb%d" % (2 + o), "qw", 128 * o, nw, 0, True, True, ["qw", nw + ".m", nw + ".m_s"])
-            act(T.yv0[:, :], T.zb0[:, 0:128], F.Copy, ["zb0"], ["yv0"])
-            cp(T.yv1[:, :], T.zb1[:, 0:128], ["zb1"], ["yv1"])
-            act(T.yw0[:, 0:128], T.zb2[:, 0:128], F.Copy, ["zb2"], ["yw0.m"])
-            cp(T.yw1[:, 0:128], T.zb3[:, 0:128], ["zb3"], ["yw1.m"])
+            products(nw, 0, nw + ".m " + nw + ".m_s")
             results(0, "yv", "")
-            tsc(T.gb[:, 131:132], T.sm[:, 2:3], 8.0, T.sm[:, 6:7], A.is_lt, A.add, ["rk", "cnt", "gb"], ["gb5"])
+            act(T.yw0[:, 0:128], T.zb2[:, 0:128], F.Copy, "zb2", "yw0.m")
+            cp(T.yw1[:, 0:128], T.zb3[:, 0:128], "zb3", "yw1.m")
+            act(T.fl[:, 32:48], T.fl[:, 16:32], F.Copy, "fm0 fm1", "fc cn", scale=2.0 ** -14, accum_out=cn)
+            act(tl[:, 994:995], cn, F.Copy, "cn gz q0", "gc", bias=1.0)
         prefill_b()
-        ni = "iw%d" % (t + 1)
         for way in (NEAR, FAR):
-            for r, n, w in seg:
+            for r, n, w, j in seg:
                 if w == way:
-                    pick(ni, K * r, K * n, iw, 0, 256, "rl%d" % t, r, inw(t, "") + [iw + ".c"], inw(t, "_s") + [iw + ".c_s"],
-                         ["rl%d.%d" % (t, way)], ni + ".m.%d" % r, ni + ".m_s.%d" % r)
+                    pick(ni, K * r, K * n, iw, 0, 256, "rl%d" % t, j, inw(t, "") + " " + iw + ".c", inw(t, "_s") + " " + iw + ".c_s",
+                         "rl%d.%d" % (t, way), ni + ".m.%d" % r, ni + ".m_s.%d" % r)
     for s, n in sorted(count.items()):
         g.wait_ge(T.sem[s], n)

from concourse.bass import DstId, RemoteDMATransfer
from concourse.mybir import dt, AluOpType as A, AxisListType, ActivationFunctionType as F

N, V, E, R, O, K = 8, 32, 128, 3, 2, 16
X4, U8, U16, BF, F32, I32 = "float8_e4m3fn_x4", "uint8", "uint16", "bfloat16", "float32", "int32"
EPS = 2.0 ** -120
BIG = 1.5 * 2.0 ** 30
SCRATCH = {}


def _buf(name, cols, dtype, where="sbuf"):
    SCRATCH[name] = (where, [128, cols], dtype)


for _i in range(4):
    _buf("zb%d" % _i, 512, F32, "psum")
    _buf("db%d" % _i, 512, F32, "psum")
for _n, _c, _d in (
        ("wr", 8, I32), ("rr", 128, I32), ("rb", 128, I32), ("mb", 1192, BF), ("tl", 1152, BF), ("wt", 1024, BF), ("eb", 520, BF), ("nb", 552, BF), ("tk", 512, BF),
        ("er", 128, BF), ("im16", 128, BF), ("ij", 128, BF), ("c32", 32, F32), ("c48", 48, F32), ("k24", 24, BF), ("oh", 48, BF), ("mk", 96, BF),
        ("ki", 12, I32), ("kf", 24, F32), ("ku", 10, U16), ("zu", 8, U16), ("ow", 6, U16), ("sg", 16, F32),
        ("li", 16, I32), ("lif", 16, F32), ("eq", 32, F32), ("ls", 16, U16), ("lf", 24, U16), ("ln", 16, U16),
        ("jk", 256, BF), ("ct", 128, F32), ("cm", 128, F32), ("th", 128, F32), ("kk", 16, F32), ("fl", 64, F32), ("hx", 24, F32),
        ("yv0", 128, F32), ("yv1", 128, F32), ("yw0", 256, F32), ("yw1", 256, F32), ("ups", 2, F32),
        ("z", 512, BF), ("dd", 512, BF), ("sx", 128, F32)):
    _buf(_n, _c, _d)
for _n, _c in (("q1", 128), ("qa", 128), ("qmb", 160), ("qc", 152), ("qb", 128), ("q3", 152), ("bb", 128), ("ep", 512), ("en", 522), ("qr", 128), ("q0", 136), ("qg", 128),
               ("qk", 128), ("qu", 128), ("qw", 256), ("qd", 128),
               ("mw0", 256), ("mw1", 256), ("mw2", 256), ("iw0", 256), ("iw1", 256), ("iw2", 128),
               ("rm0", 32), ("rc0", 64), ("rc1", 64), ("f0", 384), ("f1", 384), ("f2", 384), ("nt", 128)):
    _buf(_n, _c, X4)
    _buf(_n + "_s", _c, U8)
for _t in range(R):
    _buf("ys%d" % _t, 256, F32)
for _t in range(R - 1):
    _buf("lst%d" % _t, 16, U16)
    _buf("rl%d" % _t, 10, U16)
    _buf("rq%d" % _t, 2, U16)

STAGES = ["m0", "m0s", "c0", "c0s", "l0", "c1", "c1s", "l1"]
SEMAPHORES = ["qv", "qs", "qt", "qg", "ls", "lm", "ldr", "ldq", "lda", "ldm", "ldw", "st", "b_l0", "b_l1"]
SEMAPHORES += ["a_" + s for s in STAGES] + ["r_" + s for s in STAGES]
FAR, NEAR = 0, 1


def direct(T, topo, c):
    return [d for d in T.cores if d != c and topo.may_write(c, d)]


def cross(T, topo, c):
    return [d for d in T.cores if d != c and not topo.may_write(c, d)]


def peers(T, topo, c):
    return [x for x in topo.cores_of(c) if T.rank_of(x) is not None]


def relay(T, topo, c, d):
    own = [x for x in topo.cores_of(c) if T.rank_of(x) is None and topo.may_write(x, d)]
    near = [x for x in own if topo.die(x) == topo.die(d)] or own
    same = [x for x in cross(T, topo, c) if topo.die(x) == topo.die(d)]
    return near[same.index(d) % len(near)]


def chips(T, topo, c):
    out = []
    for d in cross(T, topo, c):
        if not out or d not in topo.cores_of(out[-1][0]):
            out.append([])
        out[-1].append(d)
    return out


def places(T, topo):
    first = T.cores[0]
    order = [d for d in T.cores if d not in cross(T, topo, first)] + cross(T, topo, first)
    return [order.index(d) for d in T.cores]


def runs(T, topo, c):
    at = places(T, topo)
    out, col = [], 0
    for x in range(N):
        d = T.cores[at.index(x)]
        if d == c:
            continue
        way = NEAR if topo.may_write(d, c) else FAR
        if out and out[-1][2] == way and out[-1][0] + out[-1][1] == x:
            out[-1][1] += 1
        else:
            out.append([x, 1, way, col + col % 2])
        col = out[-1][3] + out[-1][1]
    return out


def list_column(T, topo, s, c):
    x = places(T, topo)[T.rank_of(s)]
    return [col + x - a for a, n, _, col in runs(T, topo, c) if a <= x < a + n][0]


def pow2(n):
    k = 1
    while 2 * k <= n:
        k *= 2
    return k


def share(topo, c, dsts, spare):
    off = [d for d in dsts if d not in topo.cores_of(c)]
    on = [d for d in dsts if d in topo.cores_of(c)]
    out = {}
    every = topo.engines(c, on[0]) if on else topo.engines(c, off[0])
    per = pow2(len(every) // len(dsts))
    used = list(spare)
    for i, d in enumerate(off):
        out[d] = topo.engines(c, d)[per * i:per * i + per]
        used += out[d]
    left = [e for e in every if e not in used]
    per = pow2(len(left) // len(on)) if on else 0
    for i, d in enumerate(on):
        out[d] = left[per * i:per * i + per]
    return out


def bits(engines):
    return sum(1 << e for e in engines)


def kind(stage):
    return int(stage[1]), "_s" if stage.endswith("s") else "", stage[0] != "l" and not stage.endswith("s"), E if stage[0] == "c" else 0


def roads(T, topo, c, stage, way):
    spare = []
    if way == NEAR:
        out = [(d, [d]) for d in direct(T, topo, c)]
    elif stage[0] == "c":
        far = chips(T, topo, c)
        i = [c in ds for ds in chips(T, topo, far[0][0])].index(True)
        out = [(relay(T, topo, c, ds[(i + j + stage.endswith("s")) % len(ds)]), ds) for j, ds in enumerate(far)]
        if stage.endswith("s"):
            spare = topo.engines(c, [d for d in direct(T, topo, c) if d not in topo.cores_of(c)][0])
    else:
        out = [(relay(T, topo, c, d), [d]) for d in cross(T, topo, c)]
    e = share(topo, c, [x for x, _ in out], spare)
    return [(x, e[x], ds) for x, ds in out]


def onward(T, topo, x, stage):
    mine = peers(T, topo, x)
    ds = [r[2] for r in roads(T, topo, mine[0], stage, FAR) if r[0] == x] if mine else []
    if not ds:
        return []
    ds = ds[0]
    e = topo.engines(x, ds[0])
    if len(ds) == 1:
        return [(ds[0], e, 0, len(mine), mine[0])]
    per = pow2(len(e) // (len(mine) * len(ds)))
    out = []
    for i, s in enumerate(mine):
        for j, d in enumerate(ds):
            k = len(out)
            out.append((d, e[per * k:per * k + per], i * len(ds) + j, 1, s))
    return out


def arrival(stage, way):
    return ("b_" if stage[0] == "l" and way == FAR else "a_") + stage


def landed(T, topo, c, stage):
    n = {}
    rank = T.rank_of(c) is not None
    for s in T.cores:
        if s != c:
            for way in (FAR, NEAR):
                k = arrival(stage, way) if rank else "r_" + stage
                n[k] = n.get(k, 0) + sum(len(e) for x, e, _ in roads(T, topo, s, stage, way) if x == c)
        if rank and s == peers(T, topo, s)[0] and not topo.may_write(s, c):
            k = arrival(stage, FAR)
            n[k] = n.get(k, 0) + sum(len(o[1]) for x in topo.cores_of(s) if T.rank_of(x) is None for o in onward(T, topo, x, stage) if o[0] == c)
    return n


def view(T, name, a, n, codes):
    x = T[name][:, a:a + n]
    return x.bitcast(dt.uint8) if codes else x


def relay_program(g, core, T, topo):
    total = 0
    for st in STAGES:
        out = onward(T, topo, core, st)
        if not out:
            continue
        t, tail, codes, base = kind(st)
        tr = []
        for d, e, a, n, s in out:
            r = places(T, topo)[T.rank_of(s)]
            if st[0] == "l":
                j = list_column(T, topo, s, d)
                src, dst = T["rq%d" % t][:, a:a + n], T["rl%d" % t][:, j:j + n]
            else:
                src, dst = view(T, "r" + st[:2] + tail, K * a, K * n, codes), view(T, "iw%d" % t + tail, base + K * r, K * n, codes)
            rid, pid = topo.addr(d, core)
            tr.append(RemoteDMATransfer(dst_ids=[DstId(rid=rid, pnc=pid)], dma_engine_mask=bits(e), remote_sem=T.sem[arrival(st, FAR)], src=src, dst=dst))
            total += len(e)
        g.wait_ge(T.sem["r_" + st], landed(T, topo, core, st)["r_" + st])
        g.remote_dma_fused(tr, local_sem=T.sem["ls"])
    if total:
        g.wait_ge(T.sem["ls"], total)


def rank_program(g, core, T, topo):
    rank = T.rank_of(core)
    if rank is None:
        if peers(T, topo, core):
            relay_program(g, core, T, topo)
        return
    q = {"v": g.vector, "s": g.scalar, "t": g.tensor, "g": g, "y": g.sync}
    count, seen, wrote, read, want = {}, {}, {}, {}, {}

    def need(k, toks):
        for s, n in toks:
            if not (k == "t" and s == "qt") and seen.get((k, s), 0) < n:
                want[s] = max(want.get(s, 0), n)

    def waits(k, rd, wr):
        want.clear()
        for r in rd:
            need(k, wrote[r])
        for w in wr:
            need(k, wrote.get(w, []))
            need(k, read.get(w, []))
        for s, n in want.items():
            q[k].wait_ge(T.sem[s], n)
            seen[(k, s)] = n

    def note(tok, rd, wr):
        for r in rd:
            read.setdefault(r, []).append(tok)
        for w in wr:
            wrote[w] = [tok]
            read[w] = []

    def op(k, fn, rd, wr):
        rd, wr = rd.split(), wr.split()
        waits(k, rd, wr)
        s = "q" + k
        fn().then_inc(T.sem[s], 1)
        count[s] = count.get(s, 0) + 1
        note((s, count[s]), rd, wr)

    def dmas(parts, s, rd, wr):
        rd, wr = rd.split(), wr.split()
        for k in sorted({p[0] for p in parts}):
            waits(k, rd, wr)
        for k, o, i in parts:
            q[k].dma_start(o, i).then_inc(T.sem[s], 16)
            count[s] = count.get(s, 0) + 16
        note((s, count[s]), rd, wr)

    v, sc, te = g.vector, g.scalar, g.tensor
    u32 = dt.uint32

    def ts1(o, i, s1, o1, rd, wr):
        op("v", lambda: v.tensor_scalar(o, i, s1, None, o1), rd, wr)

    def ts2(o, i, s1, o1, s2, o2, rd, wr):
        op("v", lambda: v.tensor_scalar(o, i, s1, s2, o1, o2), rd, wr)

    def cp(o, i, rd, wr):
        op("v", lambda: v.tensor_copy(o, i), rd, wr)

    def ttn(o, a, b, f, rd, wr):
        op("v", lambda: v.tensor_tensor(o, a, b, f), rd, wr)

    def red(o, i, f, rd, wr):
        op("v", lambda: v.tensor_reduce(o, i, AxisListType.X, f), rd, wr)

    def fill(o, x, rd, wr):
        op("v", lambda: v.memset(o, x), rd, wr)

    def act(o, i, fn, rd, wr, **kw):
        op("s", lambda: sc.activation(o, i, fn, **kw), rd, wr)

    def iota(o, pattern, wr):
        op("g", lambda: g.iota(o, pattern, 0, 0, allow_small_or_imprecise_dtypes=True), "", wr)

    def quant(name, a, b, tile, x, rd, wr):
        op("v", lambda: v.quantize_mx(T[name][:, a:b], T[name + "_s"][:, a:b], T[tile][:, x:x + 4 * (b - a)]), rd, wr)

    def pickc(out, a, n, src, c, d, off, e, rd, wr):
        op("v", lambda: v.tensor_copy(T[out][:, a:a + n].bitcast(u32), T[src][:, c:d].bitcast(u32).indirect(T[off][:, e:e + n // K])), rd, wr)

    def picks(out, a, n, src, c, d, off, e, rd, wr):
        op("s", lambda: sc.activation(T[out + "_s"][:, a:a + n], T[src + "_s"][:, c:d].indirect(T[off][:, e:e + n // K]), F.Copy), rd, wr)

    def pick(out, a, n, src, c, d, off, e, codes, scales, lists, wc, ws):
        pickc(out, a, n, src, c, d, off, e, codes + " " + lists, wc)
        picks(out, a, n, src, c, d, off, e, scales + " " + lists, ws)

    def mm(bank, ln, la, rn, ra, start, stop, rd):
        op("t", lambda: te.matmul_mx(T[bank][:, 0:128], T[ln][:, la:la + 128], T[ln + "_s"][:, la:la + 128],
                                     T[rn][:, ra:ra + 128], T[rn + "_s"][:, ra:ra + 128], start, stop), rd, bank)

    def col(i):
        return T.kf[:, i:i + 1]

    def digit(i, shift, mask):
        ts2(T.ki[:, i:i + 1], T.ki[:, 0:1], shift, A.logical_shift_right, mask, A.bitwise_and, "ip", "i%d" % i)

    hc, rf, ec, n4, k8, c16, j4, k16, g16, gx, p1, hb, mx, lo, b0, b1, own, rk, ql, cn, hs = [col(i) for i in range(21)]
    tl, mb = T.tl, T.mb
    at = places(T, topo)
    place = at[rank]

    dmas([("y", T.wr[:, 0:1], T.rev[:, :])], "ldr", "", "wr")
    dmas([("s", T.rr[0:1, :], T.rev[:, :])], "ldq", "", "rr")
    dmas([("s", mb[:, 512:520], T.u[:, 0:8]), ("y", mb[:, 552:568], T.m[:, 0:16])], "lda", "", "ma")
    dmas([("y", mb[:, 568:1064], T.m[:, 16:512]), ("s", mb[:, 1064:1192], T.b[:, :])], "ldm", "", "mb")

    op("g", lambda: g.iota(T.ki[:, 0:2], [[0, 2]], 0, E + 1), "", "ip")
    iota(T.er[:, :], [[1, 16], [16, 8]], "er")
    iota(T.c32[:, :], [[128, 8], [0, 2], [2048, 2]], "c32")
    iota(T.im16[:, :], [[0, 8], [1, 16]], "im16")
    iota(T.k24[:, :], [[1, 3], [0, 8]], "k24")
    iota(T.c48[:, :], [[0, 6], [128, 8]], "c48")
    op("g", lambda: g.partition_broadcast(T.rb[:, :], T.rr[0:1, :], 128), "rr", "rb")
    steps = [K * at[4], K * at[2], K * at[1]]
    assert all(K * at[h] == steps[0] * (h // 4) + steps[1] * (h // 2 % 2) + steps[2] * (h % 2) for h in range(N))
    iota(T.sg[:, 0:8], [[x, 2] for x in steps], "sg")
    fill(T.eb[:, :], 0.0, "", "eb")
    digit(2, 3, 127)
    digit(3, 3, 124)
    digit(4, 3, 15)
    digit(5, 3, 112)
    cp(T.kf[:, 2:4], T.ki[:, 2:4], "i2 i3", "ec n4")
    digit(6, 3, 3)
    ts2(mb[:, 0:512:4], T.er[:, :], ec, A.is_gt, -1.0, A.mult, "er ec", "w0")
    ts2(mb[:, 2:512:4], T.er[:, :], ec, A.is_equal, 32.0, A.mult, "er ec", "w2")
    ts2(mb[:, 1:512:4], T.er[:, :], -3.0, A.add, n4, A.is_gt, "er n4", "w1")
    ts1(mb[:, 3:512:4], T.er[:, :], n4, A.is_ge, "er n4", "w3")
    act(tl[:, 512:608], T.eb[:, 0:96], F.Copy, "eb", "xz", scale=0.0)
    act(tl[:, 0:512], T.eb[:, 0:512], F.Copy, "eb", "cw", scale=0.0, bias=1.0)

    ts2(hc, T.wr[:, 0:1], 63.75, A.subtract, BIG, A.add, "wr", "hc")
    cp(T.kf[:, 4:7], T.ki[:, 4:7], "i4 i5 i6", "k8 c16 j4")
    ts2(mb[:, 520:552], T.c32[:, :], BIG, A.add, hc, A.is_equal, "c32 hc", "x1")
    quant("q1", 0, 128, "mb", 0, "w0 w1 w2 w3", "q1")
    quant("qa", 0, 128, "mb", 56, "w0 w1 w2 w3 ma x1", "qa")
    mm("db0", "q1", 0, "qa", 0, True, True, "q1 qa")
    act(tl[:, 512:544:4], mb[:, 520:552:4], F.Copy, "x1 k8 xz", "x2", scale=k8)
    act(tl[:, 544:576:4], mb[:, 520:552:4], F.Copy, "x1 c16 xz", "x3", scale=c16)
    cp(rf, T.wr[:, 0:1], "wr", "rf")
    ts2(hb, hc, BIG, A.subtract, -1.0 / 1024, A.mult, "hc", "hb")
    digit(7, 0, 15)
    digit(8, 4, 7)
    red(mx, T.db0[:, 116:124], A.max, "db0", "mx")
    ts2(T.mk[:, 3:96:4], T.k24[:, :], 1.0, A.add, j4, A.is_equal, "k24 j4", "mk3")
    ts2(tl[:, 0:512:4], T.im16[:, :], mx, A.add, 32.0, A.is_equal, "im16 mx", "cw")
    ts2(T.mk[:, 1:96:4], T.k24[:, :], j4, A.is_equal, -1.0, A.mult, "k24 j4", "mk1")
    quant("qc", 0, 152, "tl", 0, "cw xz x2 x3", "qc")
    mm("db1", "qc", 0, "qc", 16, True, False, "qc")
    mm("db1", "qc", 0, "qc", 24, False, True, "qc")
    quant("qmb", 0, 160, "mb", 552, "ma mb", "qmb")
    digit(9, 0, 112)
    digit(10, 0, 127)
    act(tl[:, 800:1152], T.eb[:, 0:352], F.Copy, "eb", "gz", scale=0.0)
    act(T.nb[:, 516:552], T.eb[:, 0:36], F.Copy, "eb", "xc0", scale=0.0)
    act(T.eb[:, 3:512:4], mb[:, 2:512:4], F.Copy, "w2", "eb", scale=1.0 / 32)
    act(T.mk[:, 2:96:4], T.mk[:, 3:96:4], F.Copy, "mk3", "mk2", scale=-1.0 / 32)
    cp(T.ls[:, 0:8], T.db1[:, 112:120], "db1", "ls")
    cp(T.li[:, 0:8], T.db1[:, 112:120], "db1", "li")
    pick("mw0", 0, 128, "qmb", 0, 128, "ls", 0, "qmb", "qmb", "ls", "mw0.m", "mw0.m_s")

    def send(stage, way, src, rd):
        t, tail, codes, base = kind(stage)
        i = peers(T, topo, core).index(core)
        local = "lm" if stage[0] == "m" else "ls"
        waits("g", rd, ())
        tr = []
        for x, e, ds in roads(T, topo, core, stage, way):
            n = len(ds)
            if stage[0] == "l":
                j = list_column(T, topo, core, ds[0])
                dst = T["rl%d" % t][:, j:j + 1] if way == NEAR else T["rq%d" % t][:, i:i + 1]
            elif way == NEAR:
                dst = view(T, "iw%d" % t + tail, base + K * place, K, codes)
            else:
                dst = view(T, "r" + stage[:2] + tail, K * n * i, K * n, codes)
            rid, pid = topo.addr(x, core)
            tr.append(RemoteDMATransfer(dst_ids=[DstId(rid=rid, pnc=pid)], dma_engine_mask=bits(e),
                                        remote_sem=T.sem[arrival(stage, NEAR) if way == NEAR else "r_" + stage], src=src(T.rank_of(ds[0]), n), dst=dst))
            count[local] = count.get(local, 0) + len(e)
        g.remote_dma_fused(tr, local_sem=T.sem[local])
        count.update(landed(T, topo, core, stage))

    def exchange(x):
        t, _, _, base = kind(x)
        m, part = "mw%d" % t, ".c" if base else ".m"
        for way in (FAR, NEAR):
            for st, tail in ((x, ""), (x + "s", "_s")):
                send(st, way, lambda h, n: view(T, m + tail, base + K * h, K * n, not tail), [m + part + tail])
        for st, tail in ((x, ""), (x + "s", "_s")):
            wrote["iw%d%s%s" % (t, part, tail)] = [("a_" + st, count["a_" + st])]

    exchange("m0")
    iota(T.ij[:, :], [[1, 128]], "ij")
    wrote["left"] = [("lm", count["lm"])]
    dmas([("y", T.wt[:, :], T.w[:, :])], "ldw", "left", "wt")

    def unpacking(b):
        quant("ep", 128 * b, 128 * b + 128, "eb", 3 - b, "eb", "ep%d" % b)

    def negative(b):
        quant("en", 128 * b, 128 * b + (138 if b == 3 else 128), "nb", 3 - b, "nb xc0 xc1 xc2" if b == 3 else "nb", "en%d" % b)

    ts1(T.jk[:, 0:128], T.rb[:, :], rf, A.is_lt, "rb rf", "jk")
    act(T.jk[:, 128:256], T.jk[:, 0:128], F.Identity, "jk hb", "jl lo", bias=hb, accum_out=lo)
    ttn(T.sg[:, 8:16], mb[:, 520:552:4], T.sg[:, 0:8], A.mult, "x1 sg", "sh")
    ttn(T.mk[:, 0:96:4], T.mk[:, 1:96:4], T.mk[:, 3:96:4], A.add, "mk1 mk3", "mk0")
    ts1(T.li[:, 8:16], T.li[:, 0:8], 2, A.logical_shift_right, "li", "l2")
    red(hs, T.sg[:, 8:16], A.add, "sh", "hs")
    cp(T.ow[:, 0:1], T.li[:, rank:rank + 1], "li", "ow0")
    cp(T.ls[:, 8:16], T.li[:, 8:16], "l2", "lb")
    ts1(tl[:, 704:800], T.mk[:, :], hs, A.mult, "mk0 mk1 mk2 mk3 hs", "xh")
    ts1(tl[:, 608:704], T.mk[:, :], lo, A.mult, "mk0 mk1 mk2 mk3 lo", "xl")
    act(T.lif[:, :], T.db1[:, 112:128], F.Copy, "db1 ls li", "lif")
    unpacking(0)
    quant("qb", 0, 128, "tl", 288, "cw xz x2 x3 xl xh", "qb")
    mm("db2", "q1", 0, "qb", 0, True, True, "q1 qb")
    ts2(T.oh[:, :], T.c48[:, :], BIG, A.add, hc, A.is_equal, "c48 hc", "oh")
    pick("bb", 0, 128, "qmb", 128, 160, "ls", 8, "qmb", "qmb", "lb", "bb", "bb_s")
    act(T.nb[:, 0:516], T.eb[:, 0:516], F.Copy, "eb", "nb", scale=-1.0)
    act(T.nb[:, 521:552:4], T.im16[:, 0:8], F.Copy, "im16 xc0", "xc1", scale=0.0, bias=-16.0)
    ttn(tl[:, 800:992:4], T.db2[:, 80:128], T.oh[:, :], A.mult, "db2 oh gz", "x4")
    unpacking(1)
    quant("q3", 0, 152, "tl", 384, "cw xz x2 x3 xl xh gz x4", "q3")
    mm("db3", "qc", 0, "q3", 0, True, False, "qc q3")
    mm("db3", "qc", 0, "q3", 24, False, True, "qc q3")
    unpacking(2)
    unpacking(3)
    cp(T.lf[:, :], T.db3[:, 104:128], "db3", "lf")

    def prefill_m(t):
        for b in range(4):
            mm("db%d" % b, "en", 128 * b, "mw%d" % t, 0, True, False, "en%d mw%d.m mw%d.m_s" % (b, t, t))

    def prefill_b():
        for b in range(4):
            mm("zb%d" % b, "ep", 128 * b, "bb", 0, True, False, "ep%d bb bb_s" % b)

    prefill_b()
    cp(T.kf[:, 7:11], T.ki[:, 7:11], "i7 i8 i9 i10", "k16 g16 gx p1")
    fill(T.zu[:, :], 18, "", "zu")
    pick("iw0", K * place, K, "qmb", 0, 128, "ow", 0, "qmb", "qmb", "ow0", "iw0.o", "iw0.o_s")
    ts2(T.ct[:, :], T.im16[:, :], k16, A.is_le, -2.0 ** -24, A.mult, "im16 k16", "ct")
    ts2(T.nb[:, 520:552:4], T.im16[:, 0:8], g16, A.is_equal, 256.0, A.mult, "im16 g16 xc0", "xc2")
    picks("qu", 0, 128, "qa", 96, 128, "zu", 0, "qa zu", "qu_s")
    act(T.cm[:, :], T.ct[:, :], F.Copy, "ct", "cm", bias=1.0)
    for b in (0, 1):
        negative(b)
    seg = runs(T, topo, core)

    def inw(t, tail):
        return "iw%d.o%s " % (t, tail) + ("iw0.m" + tail if t == 0 else " ".join("iw%d.m%s.%d" % (t, tail, r[0]) for r in seg))

    def results(i, src, m):
        act(T["ys%d" % i][:, 0:128], T[src + "0"][:, 0:128].indirect(T.ln[:, 0:8]), F.Copy, src + "0" + m + " ln", "ys%d.0" % i)
        cp(T["ys%d" % i][:, 128:256], T[src + "1"][:, 0:128].indirect(T.ln[:, 0:8]), src + "1" + m + " ln", "ys%d.1" % i)
        dmas([("y", T.y[:, 256 * i:256 * i + 256], T["ys%d" % i][:, :])], "st", "ys%d.0 ys%d.1" % (i, i), "")

    def natural(bank, stop):
        mm(bank, "qk", 0, "q0", 0, True, False, "qk q0")
        mm(bank, "qk", 0, "q0", 8, False, stop, "qk q0")

    def products(m, a, rd):
        for o in range(O):
            mm("zb%d" % (2 + o), "qw", 128 * o, m, a, True, True, "qw " + rd)

    for t in range(R):
        iw, mw, f = "iw%d" % t, "mw%d" % t, "f%d" % t
        nw, ni, last = "mw%d" % (t + 1), "iw%d" % (t + 1), t == R - 1
        both, both_s = mw + ".m " + mw + ".c", mw + ".m_s " + mw + ".c_s"
        for k in range(3):
            pick(f, 128 * k, 128, iw, 0, 128, "lf", 8 * k, inw(t, ""), inw(t, "_s"), "lf", f + ".%d" % k, f + "s.%d" % k)
        for k in range(3):
            for b in range(4):
                mm("zb%d" % b, "ep", 128 * b, f, 128 * k, False, k == 2, "ep%d %s.%d %ss.%d" % (b, f, k, f, k))
        if t == 0:
            for b in (2, 3):
                negative(b)
            prefill_m(0)
        if t == 1:
            quant("qw", 0, 256, "wt", 0, "wt", "qw")
        if last:
            results(1, "yw", ".m")
        for b in range(4):
            if b % 2:
                ts1(T.z[:, b:512:4], T["zb%d" % b][:, 0:128], 0.25, A.mult, "zb%d" % b, "z%d" % b)
            else:
                act(T.z[:, b:512:4], T["zb%d" % b][:, 0:128], F.Copy, "zb%d" % b, "z%d" % b, scale=0.25)
        quant(mw, 128, 256, "z", 0, "z0 z1 z2 z3", mw + ".c " + mw + ".c_s")
        for b in range(4):
            mm("db%d" % b, "ep", 128 * b, mw, 128, False, True, "ep%d %s.c" % (b, mw))
        if t == 0:
            pickc("qu", 0, 128, "qa", 96, 128, "zu", 0, "qa zu", "qu")
        if t == 1:
            products(mw, 0, mw + ".m " + mw + ".m_s")
        if last:
            products(mw, 128, mw + ".c")
        else:
            exchange("c%d" % t)
        for b in range(4):
            if b % 2:
                cp(T.dd[:, b:512:4], T["db%d" % b][:, 0:128], "db%d" % b, "dd%d" % b)
            else:
                act(T.dd[:, b:512:4], T["db%d" % b][:, 0:128], F.Copy, "db%d" % b, "dd%d" % b)
        quant("qd", 0, 128, "dd", 0, "dd0 dd1 dd2 dd3", "qd")
        if t == 1:
            natural("db0", True)
            cp(T.yv1[:, :], T.zb3[:, 0:128], "zb3", "yv1")
            act(T.yv0[:, :], T.zb2[:, 0:128], F.Copy, "zb2", "yv0")
            cp(T.ln[:, 0:8], T.db0[:, 120:128], "db0", "ln")
        if last:
            natural("db0", False)
            cp(T.yw0[:, 128:256], T.zb2[:, 0:128], "zb2", "yw0.c")
            act(T.yw1[:, 128:256], T.zb3[:, 0:128], F.Copy, "zb3", "yw1.c")
        mm("zb0", "qd", 0, "qu", 0, True, True, "qu qu_s qd")
        mm("zb1", "qu", 0, "qd", 0, True, True, "qu qu_s qd")
        if t == 0:
            ts2(T.ku[:, 0:8], T.im16[:, 0:8], 0.0, A.mult, p1, A.add, "im16 p1", "ku")
            ts1(b0, k16, float(K * place), A.add, "k16", "b0")
            ts1(b1, k16, float(K * place + E), A.add, "k16", "b1")
        act(own, T.zb0[:, 0:1], F.Abs, "zb0", "own", bias=EPS)
        act(T.sx[:, :], T.zb1[:, 0:128], F.Abs, "zb1", "sx", bias=EPS)
        if last:
            ts1(T.th[:, 0:16], T.cm[:, 0:16], own, A.mult, "cm own", "th")
            ttn(T.kk[:, :], T.sx[:, :].indirect(T.ku[:, 0:1]), T.th[:, 0:16], A.is_gt, "sx ku th", "kk")
            red(rk, T.kk[:, :], A.add, "kk", "rk")
            ts2(tl[:, 1056:1088:4], T.hx[:, 8:16], rk, A.is_gt, 128.0, A.mult, "hx rk gz", "gf")
            act(tl[:, 993:994], rk, F.Sign, "rk gz", "gs", scale=-1.0, bias=8.5)
            quant("qg", 0, 128, "tl", 576, "xz xl xh gz x4 gf gs gc", "qg")
            mm("db0", "qk", 0, "qg", 0, False, True, "qk qg")
            cp(T.ln[:, 8:16], T.db0[:, 120:128], "db0", "nl")
            cp(T.ups[:, 0:1], T.db0[:, 104:105], "db0", "ups")
            pick("nt", 0, 128, mw, 0, 256, "ln", 8, both, both_s, "nl", "nt", "nt_s")
            act(T.ys2[:, 0:128], T.yw0[:, :].indirect(T.ln[:, 8:16]), F.Copy, "yw0.m yw0.c nl", "ys2.0")
            cp(T.ys2[:, 128:256], T.yw1[:, :].indirect(T.ln[:, 8:16]), "yw1.m yw1.c nl", "ys2.1")
            planes = [("yyss"[k], T.osc[4 * k:4 * k + 4, :], T["nt_s"][32 * k:32 * k + 4, :]) for k in range(4)]
            dmas([("y", T.up[:, :], T.ups[:, 0:1])], "st", "ups", "")
            dmas([("y", T.oc[:, :], view(T, "nt", 0, 128, True))], "st", "nt", "")
            dmas(planes[:2], "st", "nt_s", "")
            dmas([("s", T.y[:, 512:640], T.ys2[:, 0:128])], "st", "ys2.0", "")
            dmas([("y", T.y[:, 640:768], T.ys2[:, 128:256])], "st", "ys2.1", "")
            dmas(planes[2:], "st", "nt_s", "")
            break
        lst = "lst%d" % t
        ts1(T.th[:, :], T.cm[:, :], own, A.mult, "cm own", "th")
        ttn(tl[:, 0:512:4], T.sx[:, :].indirect(T.ku[:, 0:8]), T.th[:, :], A.is_gt, "sx ku th", "cw")
        quant("qr", 0, 128, "tl", 0, "cw", "qr")
        mm("zb2", "qr", 0, "en", 394, True, True, "qr en3")
        if t == 0:
            ts2(T.fl[:, 48:56], T.im16[:, 0:8], 16.0, A.mult, k16, A.add, "im16 k16", "pb")
            cp(T.ku[:, 8:9], T.ki[:, 8:9], "i8", "kg")
        ts2(T[lst][:, 0:8], T.zb2[:, 120:128], b0, A.max, b1, A.min, "zb2 b0 b1", lst)
        for way in (FAR, NEAR):
            send("l%d" % t, way, lambda h, n: T[lst][:, h:h + n], [lst])
        for way in (FAR, NEAR):
            s = arrival("l%d" % t, way)
            wrote["rl%d.%d" % (t, way)] = [(s, count[s])]
        ts2(T.fl[:, 0:8], T.zb2[:, 120:128], 128.0, A.is_gt, 128.0, A.mult, "zb2", "fa")
        if t == 0:
            cp(T.eq[:, 0:16], T.lif[:, 0:8].indirect(T.ku[:, 8:9]), "lif kg", "e0")
            act(T.eq[:, 16:32], T.lif[:, 8:16].indirect(T.ku[:, 8:9]), F.Copy, "lif kg", "e1")
        ttn(T.fl[:, 8:16], T.fl[:, 0:8], T.fl[:, 48:56], A.add, "fa pb", "fb")
        ttn(T.fl[:, 16 + 8 * t:24 + 8 * t], T.fl[:, 0:8], T.nb[:, 520:552:4], A.mult, "fa xc2", "fm%d" % t)
        cp(T[lst][:, 8:16], T.fl[:, 8:16], "fb", lst + "o")
        cp(T.ow[:, 2 * t + 2:2 * t + 3], T.fl[:, 8 + rank:9 + rank], "fb", "ow%d" % (t + 1))
        if t == 0:
            ttn(ql, T.eq[:, 0:1], T.eq[:, 16:17], A.subtract, "e0 e1", "ql")
        pick(nw, 0, 128, mw, 0, 256, lst, 8, both, both_s, lst + "o", nw + ".m", nw + ".m_s")
        prefill_m(t + 1)
        pick(ni, K * place, K, mw, 0, 256, "ow", 2 * t + 2, both, both_s, "ow%d" % (t + 1), ni + ".o", ni + ".o_s")
        if t == 0:
            ts1(T.tk[:, 0:512:4], T.im16[:, :], ql, A.is_equal, "im16 ql", "tk0")
            ts2(T.tk[:, 1:512:4], T.ij[:, :], T.eq[:, 0:1], A.is_equal, 0.5, A.mult, "ij e0", "tk1")
            ts2(T.hx[:, 0:8], T.im16[:, 0:8], 16.0, A.mult, T.eq[:, 16:17], A.is_equal, "im16 e1", "ho")
            for i in (2, 3):
                act(T.tk[:, i:512:4], T.tk[:, 1:512:4], F.Copy, "tk1", "tk%d" % i)
            act(tl[:, 1088:1120:4], T.hx[:, 0:8], F.Copy, "ho k16 gz", "g1", scale=k16)
            act(tl[:, 1120:1152:4], T.hx[:, 0:8], F.Copy, "ho gx gz", "g2", scale=gx)
            act(T.hx[:, 8:16], T.hx[:, 0:8], F.Copy, "ho", "hx", scale=9.0)
            quant("qk", 0, 128, "tk", 0, "tk0 tk1 tk2 tk3", "qk")
            quant("q0", 0, 136, "tl", 608, "xl xh gz x4 g1 g2", "q0")
        else:
            products(nw, 0, nw + ".m " + nw + ".m_s")
            results(0, "yv", "")
            act(T.yw0[:, 0:128], T.zb2[:, 0:128], F.Copy, "zb2", "yw0.m")
            cp(T.yw1[:, 0:128], T.zb3[:, 0:128], "zb3", "yw1.m")
            act(T.fl[:, 32:48], T.fl[:, 16:32], F.Copy, "fm0 fm1", "fc cn", scale=2.0 ** -14, accum_out=cn)
            act(tl[:, 994:995], cn, F.Copy, "cn gz q0", "gc", bias=1.0)
        prefill_b()
        for way in (NEAR, FAR):
            for r, n, w, j in seg:
                if w == way:
                    pick(ni, K * r, K * n, iw, 0, 256, "rl%d" % t, j, inw(t, "") + " " + iw + ".c", inw(t, "_s") + " " + iw + ".c_s",
                         "rl%d.%d" % (t, way), ni + ".m.%d" % r, ni + ".m_s.%d" % r)
    for s, n in sorted(count.items()):
        g.wait_ge(T.sem[s], n)
